import numpy as np
import ml_dtypes


def mxq(x, axis, fmt="e4m3"):
    dtype, down = {"e4m3": (ml_dtypes.float8_e4m3fn, 7), "e5m2": (ml_dtypes.float8_e5m2, 14)}[fmt]
    v = np.moveaxis(np.asarray(x, np.float32).astype(ml_dtypes.bfloat16).astype(np.float64), axis, -1)
    blocks = v.reshape(v.shape[:-1] + (-1, 32))
    amax = np.abs(blocks).max(-1, keepdims=True)
    byte = np.maximum(np.where(amax > 0, np.frexp(amax)[1] - 1 + 127, 0) - down, 1)
    scale = np.exp2(byte - 127.0)
    codes = (blocks / scale).astype(np.float32).astype(dtype).astype(np.float64)
    return np.moveaxis((codes * scale).reshape(v.shape), -1, axis)


WIDE = False


def mx_kscale(k):
    if not WIDE:
        return np.ones(k)
    levels = np.array([10, -10, 5, -5, 0])
    if k % 512:
        return np.exp2(np.random.permutation(np.resize(levels, k // 32))).repeat(32)
    a = np.empty((k // 512, 16))
    for p in range(k // 512):
        a[p, :8] = np.random.permutation(np.resize(levels, 8))
        for g in range(8):
            far = levels[np.abs(levels - a[p, g]) >= 10]
            a[p, g + 8] = far[np.random.randint(len(far))]
    return np.exp2(a.ravel()).repeat(32)


def f64(x):
    return np.asarray(x).astype(np.float64)


def striped(idx):
    return np.tile(idx.reshape(-1, 16).T, (8, 1)).astype(np.uint16)


def unstriped(offs):
    return offs[:16].T.reshape(-1).astype(np.int64)


def pack_weight(w):
    k, n = w.shape
    w = f64(np.asarray(w, np.float32).astype(ml_dtypes.bfloat16)).reshape(k // 32, 32, n)
    amax = np.abs(w).max(1)
    byte = np.clip(np.where(amax > 0, np.frexp(amax)[1] - 1 + 127 - 7, 1), 1, 254)
    scaled = (w * np.exp2(127.0 - byte)[:, None, :]).reshape(k, n).astype(np.float32)
    words = np.ascontiguousarray(scaled.reshape(k // 512, 128, 4, n).transpose(0, 1, 3, 2)).astype(ml_dtypes.float8_e4m3fn).view(np.uint8)
    return words, np.ascontiguousarray(byte.astype(np.uint8).reshape(k // 512, 16, n))


def unpack_weight(words, scales):
    g, p, n, _ = words.shape
    vals = np.ascontiguousarray(words).view(ml_dtypes.float8_e4m3fn).astype(np.float64) * np.repeat(np.exp2(scales.astype(np.float64) - 127.0), 8, axis=1)[..., None]
    return vals.transpose(0, 1, 3, 2).reshape(g * 512, n)


def relu(v):
    return np.maximum(v, 0.0)


K, T, S, H, D, V, W, U = 1024, 1024, 512, 512, 8, 128, 2048, 1024
P = 2 ** 7


def setup_inputs():
    n = np.random.standard_normal
    s = mx_kscale(K)[:, None]
    u = mx_kscale(H)
    packed_xT = pack_weight(n((K, T)) * s)
    packed_eT = pack_weight(n((H, W)) / np.sqrt(H) / u[:, None])
    return {
        "x_words": packed_xT[0],
        "x_scales": packed_xT[1],
        "w1": (n((K, H)) / np.sqrt(K) / s * u).astype(np.float32),
        "e_words": packed_eT[0],
        "e_scales": packed_eT[1],
        "nb": (np.tile(np.random.uniform(0.5, 1.5, W), (P, 1))).astype(np.float32),
        "own": (np.random.uniform(0.5, 1.5, (S, 1))).astype(np.float32),
        "cnt": (np.tile(np.random.uniform(0.3, 1.0, V), (P, 1))).astype(np.float32),
        "offs": striped(np.random.permutation(T)[:S]),
        "oth": striped(np.random.permutation(W)[:U]),
    }


def reference(x_words, x_scales, w1, e_words, e_scales, nb, own, cnt, offs, oth):
    xq = unpack_weight(x_words, x_scales)[:, unstriped(offs)]
    h = mxq(f64(w1), 0, "e4m3").T @ xq
    e_oth = unpack_weight(e_words, e_scales)[:, unstriped(oth)]
    y = mxq(h, 0, "e4m3").T @ e_oth
    dd = f64(nb)[:1][:, unstriped(oth)] - y
    near = dd.reshape(len(dd), -1, D).min(axis=2)
    rr = near + f64(own)
    return -1.0 * ((np.exp(-1.0 * relu(rr))) * f64(cnt)[:1]) + 1.0

@@ -1,0 +1,190 @@
+from contextlib import ExitStack
+
+import concourse.mybir as mybir
+from concourse.masks import make_identity
+
+K, T, S, H, D, V, W, U = 1024, 1024, 512, 512, 8, 128, 2048, 1024
+FLOPS = 2 * K * H * S + 2 * H * S * U
+
+F32 = mybir.dt.float32
+BF16 = mybir.dt.bfloat16
+I32 = mybir.dt.int32
+U32 = mybir.dt.uint32
+U16 = mybir.dt.uint16
+U8 = mybir.dt.uint8
+FP8X4 = mybir.dt.float8_e4m3fn_x4
+ALU = mybir.AluOpType
+ACT = mybir.ActivationFunctionType
+
+P = 128
+PACK = 4
+PASSES = K // 512
+BANK = 512
+HALF = S // 2
+
+
+def tile_picked_ycham_dens_p_kernel(
+    tc, x_words, x_scales, w1, e_words, e_scales, nb, own, cnt, offs, oth, out
+):
+    nc = tc.nc
+    with ExitStack() as ctx:
+        keep = ctx.enter_context(tc.tile_pool(name="keep", bufs=1))
+        psum = ctx.enter_context(tc.psum_pool(name="psum", bufs=8))
+
+        offs_t = keep.tile([P, S // 16], U16, name="offs_t")
+        oth_t = keep.tile([P, U // 16], U16, name="oth_t")
+        xs_tab = keep.tile([P, T], U8, name="xs_tab", align_bytes=64)
+        es_tab = keep.tile([P, W], U8, name="es_tab", align_bytes=64)
+        nb_tab = keep.tile([P, W], F32, name="nb_tab", align_bytes=64)
+        xw_tab = [keep.tile([P, T], I32, name="xw_tab%d" % g, align_bytes=64) for g in range(PASSES)]
+        ew_tab = keep.tile([P, W], I32, name="ew_tab", align_bytes=64)
+        w_raw = [[keep.tile([P, PACK, H // 2], F32, name="w_raw%d%d" % (g, u), align_bytes=64) for u in range(2)]
+                 for g in range(PASSES)]
+        own_t = keep.tile([P, S // P], F32, name="own_t")
+        cnt_t = keep.tile([P, V], F32, name="cnt_t")
+        ident = keep.tile([P, P], F32, name="ident", align_bytes=64)
+        zero = keep.tile([P, 1], F32, name="zero")
+        one = keep.tile([P, 1], F32, name="one")
+
+        nc.gpsimd.memset(xs_tab[:].bitcast(I32), 0)
+        nc.vector.memset(nb_tab[:], 0.0)
+        nc.gpsimd.memset(zero[:], 0.0)
+        nc.scalar.activation(one[:], zero[:], ACT.Exp)
+        make_identity(nc, ident[:])
+        nc.gpsimd.memset(es_tab[:].bitcast(I32), 0)
+
+        def load_w(g, u):
+            nc.sync.dma_start(
+                w_raw[g][u][:],
+                w1[512 * g:512 * (g + 1), 256 * u:256 * (u + 1)].rearrange("(p j) c -> p j c", j=PACK),
+            )
+
+        def load_words(tab, words):
+            nc.sync.dma_start(tab[:], words.rearrange("p n t -> p (n t)").bitcast(I32))
+
+        nc.sync.dma_start(offs_t[:], offs)
+        for q in range(4):
+            nc.sync.dma_start(xs_tab[32 * q:32 * q + 8, :].bitcast(I32), x_scales[:, 4 * q:4 * q + 4, :].bitcast(I32))
+        load_w(0, 0)
+        nc.sync.dma_start(oth_t[:], oth)
+        nc.sync.dma_start(nb_tab[0:1, :], nb[0:1, :])
+        load_w(0, 1)
+        load_words(xw_tab[0], x_words[0])
+        for q in range(4):
+            nc.sync.dma_start(es_tab[32 * q:32 * q + 4, :].bitcast(I32), e_scales[0, 4 * q:4 * q + 4, :].bitcast(I32))
+        load_w(1, 0)
+        load_w(1, 1)
+        load_words(xw_tab[1], x_words[1])
+        load_words(ew_tab, e_words[0])
+        nc.sync.dma_start(cnt_t[:], cnt)
+        with nc.allow_non_contiguous_dma(reason="one value a partition"):
+            nc.sync.dma_start(own_t[:], own.rearrange("(c p) o -> p (c o)", p=P))
+
+        xs = keep.tile([P, S], U8, name="xs", align_bytes=64)
+        es = keep.tile([P, U], U8, name="es", align_bytes=64)
+        nbg = keep.tile([P, U], F32, name="nbg", align_bytes=64)
+        xw = [keep.tile([P, S], U32, name="xw%d" % g, align_bytes=64) for g in range(PASSES)]
+        ew = keep.tile([P, U], U32, name="ew", align_bytes=64)
+        ew_d = [keep.tile([P, 4, V], U32, name="ew_d%d" % a, align_bytes=64) for a in range(2)]
+        neg_nb = keep.tile([P, D], F32, name="neg_nb")
+        w_bf = [keep.tile([P, PACK, P, PACK], BF16, name="w_bf%d" % g, tag="w_bf%d" % g, align_bytes=64) for g in range(PASSES)]
+        wc = [keep.tile([P, H], U32, name="wc%d" % g, align_bytes=64) for g in range(PASSES)]
+        ws = [keep.tile([P, H], U8, name="ws%d" % g, align_bytes=64) for g in range(PASSES)]
+        h_bf = [keep.tile([P, HALF, PACK], BF16, name="h_bf%d" % a, align_bytes=64) for a in range(2)]
+        hc = [keep.tile([P, HALF], U32, name="hc%d" % a, align_bytes=64) for a in range(2)]
+        hs = [keep.tile([P, HALF], U8, name="hs%d" % a, align_bytes=64) for a in range(2)]
+
+        def deal(dst, src, a):
+            nc.vector.tensor_copy(
+                dst.rearrange("p d v -> p v d"),
+                src[:].rearrange("p (v d) -> p v d", d=D)[:, :, 4 * a:4 * a + 4],
+            )
+
+        def cast_w(g, u):
+            nc.scalar.copy(
+                w_bf[g][:, :, 64 * u:64 * (u + 1), :].rearrange("p r m j -> p m j r"),
+                w_raw[g][u][:].rearrange("p j (m r) -> p m j r", r=PACK),
+            )
+
+        def quant_w(g):
+            nc.vector.quantize_mx(wc[g][:].bitcast(FP8X4), ws[g][:], w_bf[g][:].rearrange("p r m j -> p (r m j)"))
+
+        cast_w(0, 0)
+        cast_w(0, 1)
+        nc.vector.tensor_copy(xs[:], xs_tab[:].indirect(offs_t[:]))
+        nc.vector.tensor_copy(nbg[:], nb_tab[:].indirect(oth_t[:]))
+        for a in range(2):
+            nbb = psum.tile([P, BANK], F32, name="bank")
+            for d in range(4):
+                nc.tensor.transpose(nbb[:, P * d:P * (d + 1)], nbg[:, 4 * a + d:U:D], ident[:])
+            nc.scalar.activation(neg_nb[:, 4 * a:4 * a + 4], nbb[:, 0:BANK:P], ACT.Copy, scale=-1.0)
+
+        nc.vector.tensor_copy(xw[0][:], xw_tab[0][:].bitcast(U32).indirect(offs_t[:]))
+        quant_w(0)
+        nc.vector.tensor_copy(es[:], es_tab[:].indirect(oth_t[:]))
+        cast_w(1, 0)
+        cast_w(1, 1)
+        nc.vector.tensor_copy(xw[1][:], xw_tab[1][:].bitcast(U32).indirect(offs_t[:]))
+        quant_w(1)
+
+        for b in range(S // P):
+            hb = psum.tile([P, BANK], F32, name="bank")
+            cols = slice(P * b, P * (b + 1))
+            for r in range(PACK):
+                for g in range(PASSES):
+                    nc.tensor.matmul_mx(
+                        hb[:, P * r:P * (r + 1)],
+                        lhsT=wc[g][:, P * r:P * (r + 1)].bitcast(FP8X4), lhsT_scale=ws[g][:, P * r:P * (r + 1)],
+                        rhs=xw[g][:, cols].bitcast(FP8X4), rhs_scale=xs[4 * g:P, cols],
+                        start=(g == 0), stop=(g == PASSES - 1),
+                    )
+            nc.scalar.copy(
+                h_bf[b // 2][:, P * (b % 2):P * (b % 2 + 1), :],
+                hb[:].rearrange("p (r t) -> p t r", r=PACK),
+            )
+
+        def quant_h(a):
+            nc.vector.quantize_mx(hc[a][:].bitcast(FP8X4), hs[a][:], h_bf[a][:].rearrange("p t r -> p (t r)"))
+
+        es_d = keep.tile([P, D, V], U8, name="es_d", tag="w_bf1", align_bytes=64)
+        deal(es_d[:, 0:4, :], es, 0)
+        deal(es_d[:, 4:8, :], es, 1)
+        nc.vector.tensor_copy(ew[:], ew_tab[:].bitcast(U32).indirect(oth_t[:]))
+        deal(ew_d[0][:], ew, 0)
+        quant_h(0)
+        deal(ew_d[1][:], ew, 1)
+        quant_h(1)
+
+        for a in range(2):
+            best = [keep.tile([P, HALF], F32, name="best%d%d" % (a, c), align_bytes=64) for c in range(2)]
+            for d in range(D):
+                yb = psum.tile([P, BANK], F32, name="bank")
+                nc.tensor.matmul_mx(
+                    yb[:, 0:HALF],
+                    lhsT=ew_d[d // 4][:, d % 4, :].bitcast(FP8X4), lhsT_scale=es_d[:, d, :],
+                    rhs=hc[a][:].bitcast(FP8X4), rhs_scale=hs[a][:],
+                    start=True, stop=True,
+                )
+                if d < 2:
+                    nc.scalar.activation(best[d][:], yb[:, 0:HALF], ACT.Identity, bias=neg_nb[:, d:d + 1])
+                else:
+                    nc.vector.scalar_tensor_tensor(
+                        best[d % 2][:], yb[:, 0:HALF], neg_nb[:, d:d + 1], best[d % 2][:], ALU.add, ALU.max
+                    )
+            for c in range(2):
+                n = 2 * a + c
+                top = keep.tile([P, P], F32, name="top%d" % n, align_bytes=64)
+                nc.vector.tensor_tensor(top[:], best[0][:, P * c:P * (c + 1)], best[1][:, P * c:P * (c + 1)], ALU.max)
+                tb = psum.tile([P, BANK], F32, name="bank")
+                nc.tensor.transpose(tb[:, 0:V], top[:], ident[:])
+                rr = keep.tile([P, V], F32, name="rr%d" % n)
+                res = keep.tile([P, V], F32, name="res%d" % n)
+                nc.scalar.activation(rr[:], tb[:, 0:V], ACT.Relu, scale=-1.0, bias=own_t[:, n:n + 1])
+                nc.scalar.activation(rr[:], rr[:], ACT.Exp, scale=-1.0)
+                if a == 0:
+                    nc.gpsimd.tensor_tensor(rr[:], rr[:], cnt_t[:], ALU.mult)
+                    nc.scalar.activation(res[:], rr[:], ACT.Identity, scale=-1.0, bias=one[:])
+                else:
+                    nc.vector.tensor_tensor(rr[:], rr[:], cnt_t[:], ALU.mult)
+                    nc.vector.tensor_scalar(res[:], rr[:], -1.0, 1.0, ALU.mult, ALU.add)
+                nc.sync.dma_start(out[P * n:P * (n + 1), :], res[:])

@@ -29,7 +29,8 @@ def tile_picked_ycham_dens_p_kernel(
     nc = tc.nc
     with ExitStack() as ctx:
         keep = ctx.enter_context(tc.tile_pool(name="keep", bufs=1))
-        psum = ctx.enter_context(tc.psum_pool(name="psum", bufs=8))
+        psum = ctx.enter_context(tc.psum_pool(name="psum", bufs=6))
+        psum_t = ctx.enter_context(tc.psum_pool(name="psum_t", bufs=2))
 
         offs_t = keep.tile([P, S // 16], U16, name="offs_t")
         oth_t = keep.tile([P, U // 16], U16, name="oth_t")
@@ -37,8 +38,8 @@ def tile_picked_ycham_dens_p_kernel(
         es_tab = keep.tile([P, W], U8, name="es_tab", align_bytes=64)
         nb_tab = keep.tile([P, W], F32, name="nb_tab", align_bytes=64)
         xw_tab = [keep.tile([P, T], I32, name="xw_tab%d" % g, align_bytes=64) for g in range(PASSES)]
-        ew_tab = keep.tile([P, W], I32, name="ew_tab", align_bytes=64)
-        w_raw = [[keep.tile([P, PACK, H // 2], F32, name="w_raw%d%d" % (g, u), align_bytes=64) for u in range(2)]
+        ew_tab = keep.tile([P, W], I32, name="ew_tab", tag="ew_tab", align_bytes=64)
+        w_raw = [[keep.tile([P, PACK, H // 2], F32, name="w_raw%d%d" % (g, u), tag="w_raw%d%d" % (g, u), align_bytes=64) for u in range(2)]
                  for g in range(PASSES)]
         own_t = keep.tile([P, S // P], F32, name="own_t")
         cnt_t = keep.tile([P, V], F32, name="cnt_t")
@@ -46,7 +47,7 @@ def tile_picked_ycham_dens_p_kernel(
         zero = keep.tile([P, 1], F32, name="zero")
         one = keep.tile([P, 1], F32, name="one")
 
-        nc.gpsimd.memset(xs_tab[:].bitcast(I32), 0)
+        nc.vector.memset(xs_tab[:].bitcast(I32), 0)
         nc.vector.memset(nb_tab[:], 0.0)
         nc.gpsimd.memset(zero[:], 0.0)
         nc.scalar.activation(one[:], zero[:], ACT.Exp)
@@ -65,14 +66,14 @@ def tile_picked_ycham_dens_p_kernel(
         nc.sync.dma_start(offs_t[:], offs)
         for q in range(4):
             nc.sync.dma_start(xs_tab[32 * q:32 * q + 8, :].bitcast(I32), x_scales[:, 4 * q:4 * q + 4, :].bitcast(I32))
+        load_words(xw_tab[0], x_words[0])
         load_w(0, 0)
         nc.sync.dma_start(oth_t[:], oth)
         nc.sync.dma_start(nb_tab[0:1, :], nb[0:1, :])
         load_w(0, 1)
-        load_words(xw_tab[0], x_words[0])
+        load_w(1, 0)
         for q in range(4):
             nc.sync.dma_start(es_tab[32 * q:32 * q + 4, :].bitcast(I32), e_scales[0, 4 * q:4 * q + 4, :].bitcast(I32))
-        load_w(1, 0)
         load_w(1, 1)
         load_words(xw_tab[1], x_words[1])
         load_words(ew_tab, e_words[0])
@@ -81,17 +82,15 @@ def tile_picked_ycham_dens_p_kernel(
             nc.sync.dma_start(own_t[:], own.rearrange("(c p) o -> p (c o)", p=P))
 
         xs = keep.tile([P, S], U8, name="xs", align_bytes=64)
-        es = keep.tile([P, U], U8, name="es", align_bytes=64)
+        es_d0 = keep.tile([P, 4, V], U8, name="es_d0", align_bytes=64)
         nbg = keep.tile([P, U], F32, name="nbg", align_bytes=64)
         xw = [keep.tile([P, S], U32, name="xw%d" % g, align_bytes=64) for g in range(PASSES)]
-        ew = keep.tile([P, U], U32, name="ew", align_bytes=64)
+        ew = keep.tile([P, U], U32, name="ew", tag="ew", align_bytes=64)
         ew_d = [keep.tile([P, 4, V], U32, name="ew_d%d" % a, align_bytes=64) for a in range(2)]
-        neg_nb = keep.tile([P, D], F32, name="neg_nb")
         w_bf = [keep.tile([P, PACK, P, PACK], BF16, name="w_bf%d" % g, tag="w_bf%d" % g, align_bytes=64) for g in range(PASSES)]
         wc = [keep.tile([P, H], U32, name="wc%d" % g, align_bytes=64) for g in range(PASSES)]
         ws = [keep.tile([P, H], U8, name="ws%d" % g, align_bytes=64) for g in range(PASSES)]
-        h_bf = [keep.tile([P, HALF, PACK], BF16, name="h_bf%d" % a, align_bytes=64) for a in range(2)]
-        hc = [keep.tile([P, HALF], U32, name="hc%d" % a, align_bytes=64) for a in range(2)]
+        h_bf = [keep.tile([P, HALF, PACK], BF16, name="h_bf%d" % a, tag="h_bf%d" % a, align_bytes=64) for a in range(2)]
         hs = [keep.tile([P, HALF], U8, name="hs%d" % a, align_bytes=64) for a in range(2)]
 
         def deal(dst, src, a):
@@ -99,6 +98,12 @@ def tile_picked_ycham_dens_p_kernel(
                 dst.rearrange("p d v -> p v d"),
                 src[:].rearrange("p (v d) -> p v d", d=D)[:, :, 4 * a:4 * a + 4],
             )
+
+        def gather_es(u, tag):
+            es = keep.tile([P, U // 2], U8, name="es%d" % u, tag=tag, align_bytes=64)
+            nc.vector.tensor_copy(es[:], es_tab[:].indirect(oth_t[:, 32 * u:32 * (u + 1)]))
+            deal(es_d0[:, :, 64 * u:64 * (u + 1)], es, 0)
+            return es
 
         def cast_w(g, u):
             nc.scalar.copy(
@@ -112,20 +117,20 @@ def tile_picked_ycham_dens_p_kernel(
         cast_w(0, 0)
         cast_w(0, 1)
         nc.vector.tensor_copy(xs[:], xs_tab[:].indirect(offs_t[:]))
+        nc.vector.tensor_copy(xw[0][:], xw_tab[0][:].bitcast(U32).indirect(offs_t[:]))
         nc.vector.tensor_copy(nbg[:], nb_tab[:].indirect(oth_t[:]))
+        quant_w(0)
+        cast_w(1, 0)
+        cast_w(1, 1)
+        es0 = gather_es(0, "es0")
+        quant_w(1)
+        nc.vector.tensor_copy(xw[1][:], xw_tab[1][:].bitcast(U32).indirect(offs_t[:]))
+        neg_nb = keep.tile([P, D], F32, name="neg_nb", tag="w_raw11", align_bytes=64)
         for a in range(2):
-            nbb = psum.tile([P, BANK], F32, name="bank")
+            nbb = psum_t.tile([P, BANK], F32, name="turned")
             for d in range(4):
                 nc.tensor.transpose(nbb[:, P * d:P * (d + 1)], nbg[:, 4 * a + d:U:D], ident[:])
             nc.scalar.activation(neg_nb[:, 4 * a:4 * a + 4], nbb[:, 0:BANK:P], ACT.Copy, scale=-1.0)
-
-        nc.vector.tensor_copy(xw[0][:], xw_tab[0][:].bitcast(U32).indirect(offs_t[:]))
-        quant_w(0)
-        nc.vector.tensor_copy(es[:], es_tab[:].indirect(oth_t[:]))
-        cast_w(1, 0)
-        cast_w(1, 1)
-        nc.vector.tensor_copy(xw[1][:], xw_tab[1][:].bitcast(U32).indirect(offs_t[:]))
-        quant_w(1)
 
         for b in range(S // P):
             hb = psum.tile([P, BANK], F32, name="bank")
@@ -143,17 +148,21 @@ def tile_picked_ycham_dens_p_kernel(
                 hb[:].rearrange("p (r t) -> p t r", r=PACK),
             )
 
-        def quant_h(a):
-            nc.vector.quantize_mx(hc[a][:].bitcast(FP8X4), hs[a][:], h_bf[a][:].rearrange("p t r -> p (t r)"))
+        def quant_h(a, tag):
+            codes = keep.tile([P, HALF], U32, name="hc%d" % a, tag=tag, align_bytes=64)
+            nc.vector.quantize_mx(codes[:].bitcast(FP8X4), hs[a][:], h_bf[a][:].rearrange("p t r -> p (t r)"))
+            return codes
 
-        es_d = keep.tile([P, D, V], U8, name="es_d", tag="w_bf1", align_bytes=64)
-        deal(es_d[:, 0:4, :], es, 0)
-        deal(es_d[:, 4:8, :], es, 1)
+        es1 = gather_es(1, "w_bf1")
         nc.vector.tensor_copy(ew[:], ew_tab[:].bitcast(U32).indirect(oth_t[:]))
         deal(ew_d[0][:], ew, 0)
-        quant_h(0)
+        hc0 = quant_h(0, "ew_tab")
         deal(ew_d[1][:], ew, 1)
-        quant_h(1)
+        es_d1 = keep.tile([P, 4, V], U8, name="es_d1", tag="h_bf0", align_bytes=64)
+        for u, es in enumerate((es0, es1)):
+            deal(es_d1[:, :, 64 * u:64 * (u + 1)], es, 1)
+        es_d = [es_d0, es_d1]
+        hc = [hc0, quant_h(1, "ew")]
 
         for a in range(2):
             best = [keep.tile([P, HALF], F32, name="best%d%d" % (a, c), align_bytes=64) for c in range(2)]
@@ -161,7 +170,7 @@ def tile_picked_ycham_dens_p_kernel(
                 yb = psum.tile([P, BANK], F32, name="bank")
                 nc.tensor.matmul_mx(
                     yb[:, 0:HALF],
-                    lhsT=ew_d[d // 4][:, d % 4, :].bitcast(FP8X4), lhsT_scale=es_d[:, d, :],
+                    lhsT=ew_d[d // 4][:, d % 4, :].bitcast(FP8X4), lhsT_scale=es_d[d // 4][:, d % 4, :],
                     rhs=hc[a][:].bitcast(FP8X4), rhs_scale=hs[a][:],
                     start=True, stop=True,
                 )
@@ -175,7 +184,7 @@ def tile_picked_ycham_dens_p_kernel(
                 n = 2 * a + c
                 top = keep.tile([P, P], F32, name="top%d" % n, align_bytes=64)
                 nc.vector.tensor_tensor(top[:], best[0][:, P * c:P * (c + 1)], best[1][:, P * c:P * (c + 1)], ALU.max)
-                tb = psum.tile([P, BANK], F32, name="bank")
+                tb = psum_t.tile([P, BANK], F32, name="turned")
                 nc.tensor.transpose(tb[:, 0:V], top[:], ident[:])
                 rr = keep.tile([P, V], F32, name="rr%d" % n)
                 res = keep.tile([P, V], F32, name="res%d" % n)
@@ -183,8 +192,8 @@ def tile_picked_ycham_dens_p_kernel(
                 nc.scalar.activation(rr[:], rr[:], ACT.Exp, scale=-1.0)
                 if a == 0:
                     nc.gpsimd.tensor_tensor(rr[:], rr[:], cnt_t[:], ALU.mult)
-                    nc.scalar.activation(res[:], rr[:], ACT.Identity, scale=-1.0, bias=one[:])
+                    nc.gpsimd.tensor_scalar(res[:], rr[:], -1.0, 1.0, ALU.mult, ALU.add)
                 else:
                     nc.vector.tensor_tensor(rr[:], rr[:], cnt_t[:], ALU.mult)
-                    nc.vector.tensor_scalar(res[:], rr[:], -1.0, 1.0, ALU.mult, ALU.add)
+                    nc.vector.tensor_scalar(res[:], rr[:], -1.0, one[:], ALU.mult, ALU.add)
                 nc.sync.dma_start(out[P * n:P * (n + 1), :], res[:])

@@ -29,52 +29,47 @@ def tile_picked_ycham_dens_p_kernel(
     nc = tc.nc
     with ExitStack() as ctx:
         keep = ctx.enter_context(tc.tile_pool(name="keep", bufs=1))
-        psum = ctx.enter_context(tc.psum_pool(name="psum", bufs=6))
-        psum_t = ctx.enter_context(tc.psum_pool(name="psum_t", bufs=2))
+        psum = ctx.enter_context(tc.psum_pool(name="psum", bufs=5))
+        psum_t = ctx.enter_context(tc.psum_pool(name="psum_t", bufs=3))
 
         offs_t = keep.tile([P, S // 16], U16, name="offs_t")
         oth_t = keep.tile([P, U // 16], U16, name="oth_t")
-        xs_tab = keep.tile([P, T], U8, name="xs_tab", align_bytes=64)
+        xs_tab = keep.tile([P, T], U8, name="xs_tab", tag="xs_tab", align_bytes=64)
         es_tab = keep.tile([P, W], U8, name="es_tab", align_bytes=64)
-        nb_tab = keep.tile([P, W], F32, name="nb_tab", align_bytes=64)
-        xw_tab = [keep.tile([P, T], I32, name="xw_tab%d" % g, align_bytes=64) for g in range(PASSES)]
+        nb_tab = keep.tile([P, W], F32, name="nb_tab", tag="nb_tab", align_bytes=64)
+        xw_tab = [keep.tile([P, T], I32, name="xw_tab%d" % g, tag="xw_tab%d" % g, align_bytes=64) for g in range(PASSES)]
         ew_tab = keep.tile([P, W], I32, name="ew_tab", tag="ew_tab", align_bytes=64)
-        w_raw = [[keep.tile([P, PACK, H // 2], F32, name="w_raw%d%d" % (g, u), tag="w_raw%d%d" % (g, u), align_bytes=64) for u in range(2)]
-                 for g in range(PASSES)]
+        w_raw = [keep.tile([P, PACK, H], F32, name="w_raw%d" % g, tag="w_raw%d" % g, align_bytes=64) for g in range(PASSES)]
         own_t = keep.tile([P, S // P], F32, name="own_t")
         cnt_t = keep.tile([P, V], F32, name="cnt_t")
         ident = keep.tile([P, P], F32, name="ident", align_bytes=64)
         zero = keep.tile([P, 1], F32, name="zero")
         one = keep.tile([P, 1], F32, name="one")
 
+        nc.vector.memset(zero[:], 0.0)
+        nc.vector.memset(es_tab[:].bitcast(I32), 0)
+        nc.vector.memset(nb_tab[:].bitcast(I32), 0)
         nc.vector.memset(xs_tab[:].bitcast(I32), 0)
-        nc.vector.memset(nb_tab[:], 0.0)
-        nc.gpsimd.memset(zero[:], 0.0)
+        nc.vector.memset(ident[:], 0.0)
         nc.scalar.activation(one[:], zero[:], ACT.Exp)
-        make_identity(nc, ident[:])
-        nc.gpsimd.memset(es_tab[:].bitcast(I32), 0)
+        make_identity(nc, ident[:], nomemset=True)
 
-        def load_w(g, u):
-            nc.sync.dma_start(
-                w_raw[g][u][:],
-                w1[512 * g:512 * (g + 1), 256 * u:256 * (u + 1)].rearrange("(p j) c -> p j c", j=PACK),
-            )
+        def load_w(g):
+            nc.sync.dma_start(w_raw[g][:], w1[512 * g:512 * (g + 1), :].rearrange("(p j) c -> p j c", j=PACK))
 
         def load_words(tab, words):
             nc.sync.dma_start(tab[:], words.rearrange("p n t -> p (n t)").bitcast(I32))
 
+        nc.sync.dma_start(oth_t[:], oth)
         nc.sync.dma_start(offs_t[:], offs)
         for q in range(4):
-            nc.sync.dma_start(xs_tab[32 * q:32 * q + 8, :].bitcast(I32), x_scales[:, 4 * q:4 * q + 4, :].bitcast(I32))
-        load_words(xw_tab[0], x_words[0])
-        load_w(0, 0)
-        nc.sync.dma_start(oth_t[:], oth)
-        nc.sync.dma_start(nb_tab[0:1, :], nb[0:1, :])
-        load_w(0, 1)
-        load_w(1, 0)
-        for q in range(4):
             nc.sync.dma_start(es_tab[32 * q:32 * q + 4, :].bitcast(I32), e_scales[0, 4 * q:4 * q + 4, :].bitcast(I32))
-        load_w(1, 1)
+        load_w(0)
+        nc.sync.dma_start(nb_tab[0:1, :], nb[0:1, :])
+        for q in range(4):
+            nc.sync.dma_start(xs_tab[32 * q:32 * q + 8, :].bitcast(I32), x_scales[:, 4 * q:4 * q + 4, :].bitcast(I32))
+        load_w(1)
+        load_words(xw_tab[0], x_words[0])
         load_words(xw_tab[1], x_words[1])
         load_words(ew_tab, e_words[0])
         nc.sync.dma_start(cnt_t[:], cnt)
@@ -82,65 +77,60 @@ def tile_picked_ycham_dens_p_kernel(
             nc.sync.dma_start(own_t[:], own.rearrange("(c p) o -> p (c o)", p=P))
 
         xs = keep.tile([P, S], U8, name="xs", align_bytes=64)
-        es_d0 = keep.tile([P, 4, V], U8, name="es_d0", align_bytes=64)
+        es = keep.tile([P, U], U8, name="es", align_bytes=64)
+        es_d = keep.tile([P, 2, 4 * V], U8, name="es_d", align_bytes=64)
         nbg = keep.tile([P, U], F32, name="nbg", align_bytes=64)
-        xw = [keep.tile([P, S], U32, name="xw%d" % g, align_bytes=64) for g in range(PASSES)]
-        ew = keep.tile([P, U], U32, name="ew", tag="ew", align_bytes=64)
-        ew_d = [keep.tile([P, 4, V], U32, name="ew_d%d" % a, align_bytes=64) for a in range(2)]
+        xw0 = keep.tile([P, S], U32, name="xw0", align_bytes=64)
+        xw1 = [keep.tile([P, HALF], U32, name="xw1%d" % a, align_bytes=64) for a in range(2)]
+        ew_d = keep.tile([P, 2, 4 * V], U32, name="ew_d", align_bytes=64)
         w_bf = [keep.tile([P, PACK, P, PACK], BF16, name="w_bf%d" % g, tag="w_bf%d" % g, align_bytes=64) for g in range(PASSES)]
-        wc = [keep.tile([P, H], U32, name="wc%d" % g, align_bytes=64) for g in range(PASSES)]
         ws = [keep.tile([P, H], U8, name="ws%d" % g, align_bytes=64) for g in range(PASSES)]
         h_bf = [keep.tile([P, HALF, PACK], BF16, name="h_bf%d" % a, tag="h_bf%d" % a, align_bytes=64) for a in range(2)]
         hs = [keep.tile([P, HALF], U8, name="hs%d" % a, align_bytes=64) for a in range(2)]
 
-        def deal(dst, src, a):
-            nc.vector.tensor_copy(
-                dst.rearrange("p d v -> p v d"),
-                src[:].rearrange("p (v d) -> p v d", d=D)[:, :, 4 * a:4 * a + 4],
-            )
+        def cast_w(g):
+            for u in range(2):
+                nc.scalar.copy(
+                    w_bf[g][:, :, 64 * u:64 * (u + 1), :].rearrange("p r m j -> p m j r"),
+                    w_raw[g][:, :, 256 * u:256 * (u + 1)].rearrange("p j (m r) -> p m j r", r=PACK),
+                )
 
-        def gather_es(u, tag):
-            es = keep.tile([P, U // 2], U8, name="es%d" % u, tag=tag, align_bytes=64)
-            nc.vector.tensor_copy(es[:], es_tab[:].indirect(oth_t[:, 32 * u:32 * (u + 1)]))
-            deal(es_d0[:, :, 64 * u:64 * (u + 1)], es, 0)
-            return es
+        def quant_w(g, tag):
+            codes = keep.tile([P, H], U32, name="wc%d" % g, tag=tag, align_bytes=64)
+            nc.vector.quantize_mx(codes[:].bitcast(FP8X4), ws[g][:], w_bf[g][:].rearrange("p r m j -> p (r m j)"))
+            return codes
 
-        def cast_w(g, u):
-            nc.scalar.copy(
-                w_bf[g][:, :, 64 * u:64 * (u + 1), :].rearrange("p r m j -> p m j r"),
-                w_raw[g][u][:].rearrange("p j (m r) -> p m j r", r=PACK),
-            )
-
-        def quant_w(g):
-            nc.vector.quantize_mx(wc[g][:].bitcast(FP8X4), ws[g][:], w_bf[g][:].rearrange("p r m j -> p (r m j)"))
-
-        cast_w(0, 0)
-        cast_w(0, 1)
-        nc.vector.tensor_copy(xs[:], xs_tab[:].indirect(offs_t[:]))
-        nc.vector.tensor_copy(xw[0][:], xw_tab[0][:].bitcast(U32).indirect(offs_t[:]))
+        nc.vector.tensor_copy(es[:], es_tab[:].indirect(oth_t[:]))
+        nc.vector.tensor_copy(es_d[:].bitcast(I32), es[:].bitcast(I32).rearrange("p (v c) -> p c v", c=2))
         nc.vector.tensor_copy(nbg[:], nb_tab[:].indirect(oth_t[:]))
-        quant_w(0)
-        cast_w(1, 0)
-        cast_w(1, 1)
-        es0 = gather_es(0, "es0")
-        quant_w(1)
-        nc.vector.tensor_copy(xw[1][:], xw_tab[1][:].bitcast(U32).indirect(offs_t[:]))
-        neg_nb = keep.tile([P, D], F32, name="neg_nb", tag="w_raw11", align_bytes=64)
-        for a in range(2):
-            nbb = psum_t.tile([P, BANK], F32, name="turned")
-            for d in range(4):
-                nc.tensor.transpose(nbb[:, P * d:P * (d + 1)], nbg[:, 4 * a + d:U:D], ident[:])
-            nc.scalar.activation(neg_nb[:, 4 * a:4 * a + 4], nbb[:, 0:BANK:P], ACT.Copy, scale=-1.0)
+        cast_w(0)
+        cast_w(1)
+        wc0 = quant_w(0, "nb_tab")
+        nc.vector.tensor_copy(xs[:], xs_tab[:].indirect(offs_t[:]))
+        nc.vector.tensor_copy(xw0[:], xw_tab[0][:].bitcast(U32).indirect(offs_t[:]))
+        nc.vector.tensor_copy(xw1[0][:], xw_tab[1][:].bitcast(U32).indirect(offs_t[:, 0:16]))
+        wc = [wc0, quant_w(1, "wc1")]
+        nc.vector.tensor_copy(xw1[1][:], xw_tab[1][:].bitcast(U32).indirect(offs_t[:, 16:32]))
+        nb_row = keep.tile([1, P, 2, 4], F32, name="nb_row", tag="w_raw1", align_bytes=64)
+        for c in range(2):
+            nc.scalar.activation(
+                nb_row[:, :, c, :].rearrange("o (v e) q -> o v e q", e=4),
+                nbg[0:1, :].rearrange("o (q v c e) -> o c v e q", q=4, c=2, e=4)[:, c],
+                ACT.Copy, scale=-1.0,
+            )
+        neg_nb = keep.tile([P, 2, 4], F32, name="neg_nb", tag="neg_nb", align_bytes=64)
+        nc.sync.dma_start(neg_nb[:].rearrange("p c q -> p (c q)"), nb_row[:].rearrange("o m c q -> o m (c q)"))
 
         for b in range(S // P):
             hb = psum.tile([P, BANK], F32, name="bank")
             cols = slice(P * b, P * (b + 1))
+            moving = [xw0[:, cols], xw1[b // 2][:, P * (b % 2):P * (b % 2 + 1)]]
             for r in range(PACK):
                 for g in range(PASSES):
                     nc.tensor.matmul_mx(
                         hb[:, P * r:P * (r + 1)],
                         lhsT=wc[g][:, P * r:P * (r + 1)].bitcast(FP8X4), lhsT_scale=ws[g][:, P * r:P * (r + 1)],
-                        rhs=xw[g][:, cols].bitcast(FP8X4), rhs_scale=xs[4 * g:P, cols],
+                        rhs=moving[g].bitcast(FP8X4), rhs_scale=xs[4 * g:P, cols],
                         start=(g == 0), stop=(g == PASSES - 1),
                     )
             nc.scalar.copy(
@@ -153,47 +143,42 @@ def tile_picked_ycham_dens_p_kernel(
             nc.vector.quantize_mx(codes[:].bitcast(FP8X4), hs[a][:], h_bf[a][:].rearrange("p t r -> p (t r)"))
             return codes
 
-        es1 = gather_es(1, "w_bf1")
-        nc.vector.tensor_copy(ew[:], ew_tab[:].bitcast(U32).indirect(oth_t[:]))
-        deal(ew_d[0][:], ew, 0)
-        hc0 = quant_h(0, "ew_tab")
-        deal(ew_d[1][:], ew, 1)
-        es_d1 = keep.tile([P, 4, V], U8, name="es_d1", tag="h_bf0", align_bytes=64)
-        for u, es in enumerate((es0, es1)):
-            deal(es_d1[:, :, 64 * u:64 * (u + 1)], es, 1)
-        es_d = [es_d0, es_d1]
-        hc = [hc0, quant_h(1, "ew")]
+        nc.vector.tensor_copy(ew_d[:].rearrange("p c (v e) -> p v c e", e=4), ew_tab[:].bitcast(U32).indirect(oth_t[:]))
+        hc = [quant_h(0, "ew_tab"), quant_h(1, "h_bf0")]
 
+        best = {}
         for a in range(2):
-            best = [keep.tile([P, HALF], F32, name="best%d%d" % (a, c), align_bytes=64) for c in range(2)]
-            for d in range(D):
-                yb = psum.tile([P, BANK], F32, name="bank")
-                nc.tensor.matmul_mx(
-                    yb[:, 0:HALF],
-                    lhsT=ew_d[d // 4][:, d % 4, :].bitcast(FP8X4), lhsT_scale=es_d[d // 4][:, d % 4, :],
-                    rhs=hc[a][:].bitcast(FP8X4), rhs_scale=hs[a][:],
-                    start=True, stop=True,
-                )
-                if d < 2:
-                    nc.scalar.activation(best[d][:], yb[:, 0:HALF], ACT.Identity, bias=neg_nb[:, d:d + 1])
-                else:
-                    nc.vector.scalar_tensor_tensor(
-                        best[d % 2][:], yb[:, 0:HALF], neg_nb[:, d:d + 1], best[d % 2][:], ALU.add, ALU.max
+            for q in range(4):
+                yb = psum.tile([P, 2, HALF], F32, name="bank")
+                for c in range(2):
+                    nc.tensor.matmul_mx(
+                        yb[:, c, :],
+                        lhsT=ew_d[:, c, P * q:P * (q + 1)].bitcast(FP8X4), lhsT_scale=es_d[:, c, P * q:P * (q + 1)],
+                        rhs=hc[a][:].bitcast(FP8X4), rhs_scale=hs[a][:],
+                        start=True, stop=True,
                     )
-            for c in range(2):
-                n = 2 * a + c
-                top = keep.tile([P, P], F32, name="top%d" % n, align_bytes=64)
-                nc.vector.tensor_tensor(top[:], best[0][:, P * c:P * (c + 1)], best[1][:, P * c:P * (c + 1)], ALU.max)
-                tb = psum_t.tile([P, BANK], F32, name="turned")
-                nc.tensor.transpose(tb[:, 0:V], top[:], ident[:])
-                rr = keep.tile([P, V], F32, name="rr%d" % n)
-                res = keep.tile([P, V], F32, name="res%d" % n)
-                nc.scalar.activation(rr[:], tb[:, 0:V], ACT.Relu, scale=-1.0, bias=own_t[:, n:n + 1])
+                best[a, q] = keep.tile([P, HALF], F32, name="best%d%d" % (a, q), align_bytes=64)
+                nc.scalar.activation(best[a, q][:], yb[:, 0, :], ACT.Identity, bias=neg_nb[:, 0, q:q + 1])
+                nc.vector.scalar_tensor_tensor(
+                    best[a, q][:], yb[:, 1, :], neg_nb[:, 1, q:q + 1], best[a, q][:], ALU.add, ALU.max
+                )
+        for n in range(S // P):
+            tb = psum_t.tile([P, BANK], F32, name="turned")
+            for q in range(4):
+                nc.tensor.transpose(tb[:, P * q:P * (q + 1)], best[n // 2, q][:, P * (n % 2):P * (n % 2 + 1)], ident[:])
+            rr = keep.tile([P, V], F32, name="rr%d" % n, tag="neg_nb" if n == 0 else "rr%d" % n, align_bytes=64)
+            res = keep.tile([P, V], F32, name="res%d" % n)
+            nc.vector.tensor_reduce(rr[:], tb[:].rearrange("p (v e) -> p v e", e=4), mybir.AxisListType.X, ALU.max)
+            if n < 3:
+                nc.scalar.activation(rr[:], rr[:], ACT.Relu, scale=-1.0, bias=own_t[:, n:n + 1])
                 nc.scalar.activation(rr[:], rr[:], ACT.Exp, scale=-1.0)
-                if a == 0:
-                    nc.gpsimd.tensor_tensor(rr[:], rr[:], cnt_t[:], ALU.mult)
-                    nc.gpsimd.tensor_scalar(res[:], rr[:], -1.0, 1.0, ALU.mult, ALU.add)
-                else:
-                    nc.vector.tensor_tensor(rr[:], rr[:], cnt_t[:], ALU.mult)
-                    nc.vector.tensor_scalar(res[:], rr[:], -1.0, one[:], ALU.mult, ALU.add)
-                nc.sync.dma_start(out[P * n:P * (n + 1), :], res[:])
+            else:
+                nc.vector.tensor_scalar(rr[:], rr[:], own_t[:, n:n + 1], 0.0, ALU.subtract, ALU.min)
+                nc.scalar.activation(rr[:], rr[:], ACT.Exp)
+            if n < 2:
+                nc.gpsimd.tensor_tensor(rr[:], rr[:], cnt_t[:], ALU.mult)
+                nc.gpsimd.tensor_scalar(res[:], rr[:], -1.0, 1.0, ALU.mult, ALU.add)
+            else:
+                nc.vector.tensor_tensor(rr[:], rr[:], cnt_t[:], ALU.mult)
+                nc.vector.tensor_scalar(res[:], rr[:], -1.0, one[:], ALU.mult, ALU.add)
+            nc.sync.dma_start(out[P * n:P * (n + 1), :], res[:])

@@ -29,8 +29,8 @@ def tile_picked_ycham_dens_p_kernel(
     nc = tc.nc
     with ExitStack() as ctx:
         keep = ctx.enter_context(tc.tile_pool(name="keep", bufs=1))
-        psum = ctx.enter_context(tc.psum_pool(name="psum", bufs=5))
-        psum_t = ctx.enter_context(tc.psum_pool(name="psum_t", bufs=3))
+        reuse = ctx.enter_context(tc.tile_pool(name="reuse", bufs=1))
+        psum = ctx.enter_context(tc.psum_pool(name="psum", bufs=1))
 
         offs_t = keep.tile([P, S // 16], U16, name="offs_t")
         oth_t = keep.tile([P, U // 16], U16, name="oth_t")
@@ -41,7 +41,8 @@ def tile_picked_ycham_dens_p_kernel(
         ew_tab = keep.tile([P, W], I32, name="ew_tab", tag="ew_tab", align_bytes=64)
         w_raw = [keep.tile([P, PACK, H], F32, name="w_raw%d" % g, tag="w_raw%d" % g, align_bytes=64) for g in range(PASSES)]
         own_t = keep.tile([P, S // P], F32, name="own_t")
-        cnt_t = keep.tile([P, V], F32, name="cnt_t")
+        cnt_t = reuse.tile([P, V], F32, name="cnt_t", offset=2048, align_bytes=64)
+        neg_cnt = keep.tile([P, V], F32, name="neg_cnt")
         ident = keep.tile([P, P], F32, name="ident", align_bytes=64)
         zero = keep.tile([P, 1], F32, name="zero")
         one = keep.tile([P, 1], F32, name="one")
@@ -82,11 +83,10 @@ def tile_picked_ycham_dens_p_kernel(
         nbg = keep.tile([P, U], F32, name="nbg", align_bytes=64)
         xw0 = keep.tile([P, S], U32, name="xw0", align_bytes=64)
         xw1 = [keep.tile([P, HALF], U32, name="xw1%d" % a, align_bytes=64) for a in range(2)]
-        ew_d = keep.tile([P, 2, 4 * V], U32, name="ew_d", align_bytes=64)
         w_bf = [keep.tile([P, PACK, P, PACK], BF16, name="w_bf%d" % g, tag="w_bf%d" % g, align_bytes=64) for g in range(PASSES)]
         ws = [keep.tile([P, H], U8, name="ws%d" % g, align_bytes=64) for g in range(PASSES)]
         h_bf = [keep.tile([P, HALF, PACK], BF16, name="h_bf%d" % a, tag="h_bf%d" % a, align_bytes=64) for a in range(2)]
-        hs = [keep.tile([P, HALF], U8, name="hs%d" % a, align_bytes=64) for a in range(2)]
+        hc = [keep.tile([P, HALF], U32, name="hc%d" % a, align_bytes=64) for a in range(2)]
 
         def cast_w(g):
             for u in range(2):
@@ -106,6 +106,14 @@ def tile_picked_ycham_dens_p_kernel(
         cast_w(0)
         cast_w(1)
         wc0 = quant_w(0, "nb_tab")
+        warm = psum.tile([P, BANK], F32, name="warm", tag="bank4")
+        for r in range(PACK):
+            nc.tensor.matmul_mx(
+                warm[:],
+                lhsT=wc0[:, P * r:P * (r + 1)].bitcast(FP8X4), lhsT_scale=ws[0][:, P * r:P * (r + 1)],
+                rhs=wc0[:].bitcast(FP8X4), rhs_scale=ws[0][:],
+                start=True, stop=True,
+            )
         nc.vector.tensor_copy(xs[:], xs_tab[:].indirect(offs_t[:]))
         nc.vector.tensor_copy(xw0[:], xw_tab[0][:].bitcast(U32).indirect(offs_t[:]))
         nc.vector.tensor_copy(xw1[0][:], xw_tab[1][:].bitcast(U32).indirect(offs_t[:, 0:16]))
@@ -122,7 +130,7 @@ def tile_picked_ycham_dens_p_kernel(
         nc.sync.dma_start(neg_nb[:].rearrange("p c q -> p (c q)"), nb_row[:].rearrange("o m c q -> o m (c q)"))
 
         for b in range(S // P):
-            hb = psum.tile([P, BANK], F32, name="bank")
+            hb = psum.tile([P, BANK], F32, name="hb", tag="bank%d" % b)
             cols = slice(P * b, P * (b + 1))
             moving = [xw0[:, cols], xw1[b // 2][:, P * (b % 2):P * (b % 2 + 1)]]
             for r in range(PACK):
@@ -138,22 +146,34 @@ def tile_picked_ycham_dens_p_kernel(
                 hb[:].rearrange("p (r t) -> p t r", r=PACK),
             )
 
-        def quant_h(a, tag):
-            codes = keep.tile([P, HALF], U32, name="hc%d" % a, tag=tag, align_bytes=64)
-            nc.vector.quantize_mx(codes[:].bitcast(FP8X4), hs[a][:], h_bf[a][:].rearrange("p t r -> p (t r)"))
-            return codes
+        def quant_h(a):
+            scales = reuse.tile([P, HALF], U8, name="hs%d" % a, offset=2112 + HALF * a, align_bytes=64)
+            nc.vector.quantize_mx(hc[a][:].bitcast(FP8X4), scales[:], h_bf[a][:].rearrange("p t r -> p (t r)"))
+            return scales
 
-        nc.vector.tensor_copy(ew_d[:].rearrange("p c (v e) -> p v c e", e=4), ew_tab[:].bitcast(U32).indirect(oth_t[:]))
-        hc = [quant_h(0, "ew_tab"), quant_h(1, "h_bf0")]
+        def gather_ew(words, u):
+            nc.vector.tensor_copy(
+                words[:].rearrange("p c (v e) -> p v c e", e=4),
+                ew_tab[:].bitcast(U32).indirect(oth_t[:, 32 * u:32 * (u + 1)]),
+            )
+
+        ew_d0 = keep.tile([P, 2, 2 * V], U32, name="ew_d0", align_bytes=64)
+        gather_ew(ew_d0, 0)
+        nc.vector.tensor_scalar(neg_cnt[:], cnt_t[:], -1.0, None, ALU.mult)
+        hs0 = quant_h(0)
+        ew_d1 = reuse.tile([P, 2, 2 * V], U32, name="ew_d1", offset=64, align_bytes=64)
+        gather_ew(ew_d1, 1)
+        hs = [hs0, quant_h(1)]
+        ew_d = [ew_d0, ew_d1]
 
         best = {}
         for a in range(2):
             for q in range(4):
-                yb = psum.tile([P, 2, HALF], F32, name="bank")
+                yb = psum.tile([P, 2, HALF], F32, name="yb", tag="bank%d" % (q + 4 * (1 - a)))
                 for c in range(2):
                     nc.tensor.matmul_mx(
                         yb[:, c, :],
-                        lhsT=ew_d[:, c, P * q:P * (q + 1)].bitcast(FP8X4), lhsT_scale=es_d[:, c, P * q:P * (q + 1)],
+                        lhsT=ew_d[q // 2][:, c, P * (q % 2):P * (q % 2 + 1)].bitcast(FP8X4), lhsT_scale=es_d[:, c, P * q:P * (q + 1)],
                         rhs=hc[a][:].bitcast(FP8X4), rhs_scale=hs[a][:],
                         start=True, stop=True,
                     )
@@ -163,10 +183,10 @@ def tile_picked_ycham_dens_p_kernel(
                     best[a, q][:], yb[:, 1, :], neg_nb[:, 1, q:q + 1], best[a, q][:], ALU.add, ALU.max
                 )
         for n in range(S // P):
-            tb = psum_t.tile([P, BANK], F32, name="turned")
+            tb = psum.tile([P, BANK], F32, name="tb", tag="bank%d" % n)
             for q in range(4):
                 nc.tensor.transpose(tb[:, P * q:P * (q + 1)], best[n // 2, q][:, P * (n % 2):P * (n % 2 + 1)], ident[:])
-            rr = keep.tile([P, V], F32, name="rr%d" % n, tag="neg_nb" if n == 0 else "rr%d" % n, align_bytes=64)
+            rr = keep.tile([P, V], F32, name="rr%d" % n)
             res = keep.tile([P, V], F32, name="res%d" % n)
             nc.vector.tensor_reduce(rr[:], tb[:].rearrange("p (v e) -> p v e", e=4), mybir.AxisListType.X, ALU.max)
             if n < 3:
@@ -176,9 +196,9 @@ def tile_picked_ycham_dens_p_kernel(
                 nc.vector.tensor_scalar(rr[:], rr[:], own_t[:, n:n + 1], 0.0, ALU.subtract, ALU.min)
                 nc.scalar.activation(rr[:], rr[:], ACT.Exp)
             if n < 2:
-                nc.gpsimd.tensor_tensor(rr[:], rr[:], cnt_t[:], ALU.mult)
-                nc.gpsimd.tensor_scalar(res[:], rr[:], -1.0, 1.0, ALU.mult, ALU.add)
+                nc.gpsimd.tensor_tensor(rr[:], rr[:], neg_cnt[:], ALU.mult)
+                nc.gpsimd.tensor_scalar(res[:], rr[:], 1.0, 1.0, ALU.mult, ALU.add)
             else:
-                nc.vector.tensor_tensor(rr[:], rr[:], cnt_t[:], ALU.mult)
-                nc.vector.tensor_scalar(res[:], rr[:], -1.0, one[:], ALU.mult, ALU.add)
+                nc.vector.tensor_tensor(rr[:], rr[:], neg_cnt[:], ALU.mult)
+                nc.vector.tensor_scalar(res[:], rr[:], one[:], None, ALU.add)
             nc.sync.dma_start(out[P * n:P * (n + 1), :], res[:])

@@ -3,7 +3,7 @@ from contextlib import ExitStack
 import concourse.mybir as mybir
 from concourse.masks import make_identity
 
-K, T, S, H, D, V, W, U = 1024, 1024, 512, 512, 8, 128, 2048, 1024
+K, T, S, H, V, W, U = 1024, 1024, 512, 512, 128, 2048, 1024
 FLOPS = 2 * K * H * S + 2 * H * S * U
 
 F32 = mybir.dt.float32
@@ -18,9 +18,17 @@ ACT = mybir.ActivationFunctionType
 
 P = 128
 PACK = 4
-PASSES = K // 512
+PASSES = K // (P * PACK)
 BANK = 512
 HALF = S // 2
+QUARTERS = 4
+SIDES = 2
+SIDE = 4
+
+CNT_AT = 2048
+EW_B_AT = CNT_AT + 64 - 2048
+HS_AT = CNT_AT + 64
+ES_D_AT = HS_AT + 2 * HALF
 
 
 def tile_picked_ycham_dens_p_kernel(
@@ -34,21 +42,21 @@ def tile_picked_ycham_dens_p_kernel(
 
         offs_t = keep.tile([P, S // 16], U16, name="offs_t")
         oth_t = keep.tile([P, U // 16], U16, name="oth_t")
-        xs_tab = keep.tile([P, T], U8, name="xs_tab", tag="xs_tab", align_bytes=64)
+        xs_tab = keep.tile([P, T], U8, name="xs_tab", align_bytes=64)
         es_tab = keep.tile([P, W], U8, name="es_tab", align_bytes=64)
         nb_tab = keep.tile([P, W], F32, name="nb_tab", tag="nb_tab", align_bytes=64)
-        xw_tab = [keep.tile([P, T], I32, name="xw_tab%d" % g, tag="xw_tab%d" % g, align_bytes=64) for g in range(PASSES)]
-        ew_tab = keep.tile([P, W], I32, name="ew_tab", tag="ew_tab", align_bytes=64)
+        xw_tab = [keep.tile([P, T], I32, name="xw_tab%d" % g, align_bytes=64) for g in range(PASSES)]
+        ew_tab = keep.tile([P, W], I32, name="ew_tab", align_bytes=64)
         w_raw = [keep.tile([P, PACK, H], F32, name="w_raw%d" % g, tag="w_raw%d" % g, align_bytes=64) for g in range(PASSES)]
         own_t = keep.tile([P, S // P], F32, name="own_t")
-        cnt_t = reuse.tile([P, V], F32, name="cnt_t", offset=2048, align_bytes=64)
+        cnt_t = reuse.tile([P, 2, V], F32, name="cnt_t", offset=CNT_AT, align_bytes=64)
         neg_cnt = keep.tile([P, V], F32, name="neg_cnt")
         ident = keep.tile([P, P], F32, name="ident", align_bytes=64)
         zero = keep.tile([P, 1], F32, name="zero")
         one = keep.tile([P, 1], F32, name="one")
 
-        nc.vector.memset(zero[:], 0.0)
         nc.vector.memset(es_tab[:].bitcast(I32), 0)
+        nc.vector.memset(zero[:], 0.0)
         nc.vector.memset(nb_tab[:].bitcast(I32), 0)
         nc.vector.memset(xs_tab[:].bitcast(I32), 0)
         nc.vector.memset(ident[:], 0.0)
@@ -63,36 +71,38 @@ def tile_picked_ycham_dens_p_kernel(
 
         nc.sync.dma_start(oth_t[:], oth)
         nc.sync.dma_start(offs_t[:], offs)
-        for q in range(4):
-            nc.sync.dma_start(es_tab[32 * q:32 * q + 4, :].bitcast(I32), e_scales[0, 4 * q:4 * q + 4, :].bitcast(I32))
+        for quad in range(4):
+            nc.sync.dma_start(
+                es_tab[32 * quad:32 * quad + 4, :].bitcast(I32), e_scales[0, 4 * quad:4 * quad + 4, :].bitcast(I32)
+            )
         load_w(0)
         nc.sync.dma_start(nb_tab[0:1, :], nb[0:1, :])
-        for q in range(4):
-            nc.sync.dma_start(xs_tab[32 * q:32 * q + 8, :].bitcast(I32), x_scales[:, 4 * q:4 * q + 4, :].bitcast(I32))
+        for quad in range(4):
+            nc.sync.dma_start(
+                xs_tab[32 * quad:32 * quad + 8, :].bitcast(I32), x_scales[:, 4 * quad:4 * quad + 4, :].bitcast(I32)
+            )
         load_w(1)
         load_words(xw_tab[0], x_words[0])
         load_words(xw_tab[1], x_words[1])
         load_words(ew_tab, e_words[0])
-        nc.sync.dma_start(cnt_t[:], cnt)
-        with nc.allow_non_contiguous_dma(reason="one value a partition"):
-            nc.sync.dma_start(own_t[:], own.rearrange("(c p) o -> p (c o)", p=P))
+        nc.sync.dma_start(cnt_t[:, 0, :], cnt)
+        with nc.allow_non_contiguous_dma(reason="one value a partition and token block"):
+            nc.sync.dma_start(own_t[:], own.rearrange("(n p) o -> p (n o)", p=P))
 
         xs = keep.tile([P, S], U8, name="xs", align_bytes=64)
         es = keep.tile([P, U], U8, name="es", align_bytes=64)
-        es_d = keep.tile([P, 2, 4 * V], U8, name="es_d", align_bytes=64)
         nbg = keep.tile([P, U], F32, name="nbg", align_bytes=64)
-        xw0 = keep.tile([P, S], U32, name="xw0", align_bytes=64)
-        xw1 = [keep.tile([P, HALF], U32, name="xw1%d" % a, align_bytes=64) for a in range(2)]
-        w_bf = [keep.tile([P, PACK, P, PACK], BF16, name="w_bf%d" % g, tag="w_bf%d" % g, align_bytes=64) for g in range(PASSES)]
+        xw = [keep.tile([P, S], U32, name="xw%d" % g, align_bytes=64) for g in range(PASSES)]
+        w_bf = [keep.tile([P, PACK, P, PACK], BF16, name="w_bf%d" % g, align_bytes=64) for g in range(PASSES)]
         ws = [keep.tile([P, H], U8, name="ws%d" % g, align_bytes=64) for g in range(PASSES)]
-        h_bf = [keep.tile([P, HALF, PACK], BF16, name="h_bf%d" % a, tag="h_bf%d" % a, align_bytes=64) for a in range(2)]
+        h_bf = [keep.tile([P, HALF, PACK], BF16, name="h_bf%d" % a, align_bytes=64) for a in range(2)]
         hc = [keep.tile([P, HALF], U32, name="hc%d" % a, align_bytes=64) for a in range(2)]
 
         def cast_w(g):
-            for u in range(2):
+            for half in range(2):
                 nc.scalar.copy(
-                    w_bf[g][:, :, 64 * u:64 * (u + 1), :].rearrange("p r m j -> p m j r"),
-                    w_raw[g][:, :, 256 * u:256 * (u + 1)].rearrange("p j (m r) -> p m j r", r=PACK),
+                    w_bf[g][:, :, 64 * half:64 * (half + 1), :].rearrange("p r m j -> p m j r"),
+                    w_raw[g][:, :, 256 * half:256 * (half + 1)].rearrange("p j (m r) -> p m j r", r=PACK),
                 )
 
         def quant_w(g, tag):
@@ -101,7 +111,6 @@ def tile_picked_ycham_dens_p_kernel(
             return codes
 
         nc.vector.tensor_copy(es[:], es_tab[:].indirect(oth_t[:]))
-        nc.vector.tensor_copy(es_d[:].bitcast(I32), es[:].bitcast(I32).rearrange("p (v c) -> p c v", c=2))
         nc.vector.tensor_copy(nbg[:], nb_tab[:].indirect(oth_t[:]))
         cast_w(0)
         cast_w(1)
@@ -115,65 +124,70 @@ def tile_picked_ycham_dens_p_kernel(
                 start=True, stop=True,
             )
         nc.vector.tensor_copy(xs[:], xs_tab[:].indirect(offs_t[:]))
-        nc.vector.tensor_copy(xw0[:], xw_tab[0][:].bitcast(U32).indirect(offs_t[:]))
-        nc.vector.tensor_copy(xw1[0][:], xw_tab[1][:].bitcast(U32).indirect(offs_t[:, 0:16]))
+        nc.vector.tensor_copy(xw[0][:], xw_tab[0][:].bitcast(U32).indirect(offs_t[:]))
         wc = [wc0, quant_w(1, "wc1")]
-        nc.vector.tensor_copy(xw1[1][:], xw_tab[1][:].bitcast(U32).indirect(offs_t[:, 16:32]))
-        nb_row = keep.tile([1, P, 2, 4], F32, name="nb_row", tag="w_raw1", align_bytes=64)
-        for c in range(2):
+        for first, last in ((0, 1), (1, 2), (2, 4)):
+            nc.vector.tensor_copy(
+                xw[1][:, P * first:P * last], xw_tab[1][:].bitcast(U32).indirect(offs_t[:, 8 * first:8 * last])
+            )
+
+        nb_row = keep.tile([1, P, SIDES, QUARTERS], F32, name="nb_row", tag="w_raw1", align_bytes=64)
+        for c in range(SIDES):
             nc.scalar.activation(
-                nb_row[:, :, c, :].rearrange("o (v e) q -> o v e q", e=4),
-                nbg[0:1, :].rearrange("o (q v c e) -> o c v e q", q=4, c=2, e=4)[:, c],
+                nb_row[:, :, c, :].rearrange("o (u e) q -> o u e q", e=SIDE),
+                nbg[0:1, :].rearrange("o (q u c e) -> o c u e q", q=QUARTERS, c=SIDES, e=SIDE)[:, c],
                 ACT.Copy, scale=-1.0,
             )
-        neg_nb = keep.tile([P, 2, 4], F32, name="neg_nb", tag="neg_nb", align_bytes=64)
+        neg_nb = keep.tile([P, SIDES, QUARTERS], F32, name="neg_nb", align_bytes=64)
         nc.sync.dma_start(neg_nb[:].rearrange("p c q -> p (c q)"), nb_row[:].rearrange("o m c q -> o m (c q)"))
 
-        for b in range(S // P):
-            hb = psum.tile([P, BANK], F32, name="hb", tag="bank%d" % b)
-            cols = slice(P * b, P * (b + 1))
-            moving = [xw0[:, cols], xw1[b // 2][:, P * (b % 2):P * (b % 2 + 1)]]
+        for n in range(S // P):
+            hb = psum.tile([P, BANK], F32, name="hb", tag="bank%d" % n)
+            cols = slice(P * n, P * (n + 1))
             for r in range(PACK):
                 for g in range(PASSES):
                     nc.tensor.matmul_mx(
                         hb[:, P * r:P * (r + 1)],
                         lhsT=wc[g][:, P * r:P * (r + 1)].bitcast(FP8X4), lhsT_scale=ws[g][:, P * r:P * (r + 1)],
-                        rhs=moving[g].bitcast(FP8X4), rhs_scale=xs[4 * g:P, cols],
+                        rhs=xw[g][:, cols].bitcast(FP8X4), rhs_scale=xs[4 * g:P, cols],
                         start=(g == 0), stop=(g == PASSES - 1),
                     )
             nc.scalar.copy(
-                h_bf[b // 2][:, P * (b % 2):P * (b % 2 + 1), :],
+                h_bf[n // 2][:, P * (n % 2):P * (n % 2 + 1), :],
                 hb[:].rearrange("p (r t) -> p t r", r=PACK),
             )
 
         def quant_h(a):
-            scales = reuse.tile([P, HALF], U8, name="hs%d" % a, offset=2112 + HALF * a, align_bytes=64)
+            scales = reuse.tile([P, HALF], U8, name="hs%d" % a, offset=HS_AT + HALF * a, align_bytes=64)
             nc.vector.quantize_mx(hc[a][:].bitcast(FP8X4), scales[:], h_bf[a][:].rearrange("p t r -> p (t r)"))
             return scales
 
-        def gather_ew(words, u):
+        def gather_ew(words, first, last):
             nc.vector.tensor_copy(
-                words[:].rearrange("p c (v e) -> p v c e", e=4),
-                ew_tab[:].bitcast(U32).indirect(oth_t[:, 32 * u:32 * (u + 1)]),
+                words.rearrange("p c (v e) -> p v c e", e=SIDE),
+                ew_tab[:].bitcast(U32).indirect(oth_t[:, 16 * first:16 * last]),
             )
 
-        ew_d0 = keep.tile([P, 2, 2 * V], U32, name="ew_d0", align_bytes=64)
-        gather_ew(ew_d0, 0)
-        nc.vector.tensor_scalar(neg_cnt[:], cnt_t[:], -1.0, None, ALU.mult)
+        ew_a = keep.tile([P, SIDES, 2 * P], U32, name="ew_a", align_bytes=64)
+        gather_ew(ew_a[:], 0, 2)
+        nc.vector.tensor_scalar(neg_cnt[:], cnt_t[:, 0, :], -1.0, None, ALU.mult)
+        es_d = reuse.tile([P, SIDES, SIDE * V], U8, name="es_d", offset=ES_D_AT, align_bytes=64)
+        nc.vector.tensor_copy(es_d[:].bitcast(I32), es[:].bitcast(I32).rearrange("p (v c) -> p c v", c=SIDES))
         hs0 = quant_h(0)
-        ew_d1 = reuse.tile([P, 2, 2 * V], U32, name="ew_d1", offset=64, align_bytes=64)
-        gather_ew(ew_d1, 1)
+        ew_b = reuse.tile([P, 2, SIDES, P], U32, name="ew_b", offset=EW_B_AT, align_bytes=64)
+        for q in (2, 3):
+            gather_ew(ew_b[:, q - 2], q, q + 1)
         hs = [hs0, quant_h(1)]
-        ew_d = [ew_d0, ew_d1]
+        ew_d = [ew_a[:, :, 0:P], ew_a[:, :, P:2 * P], ew_b[:, 0], ew_b[:, 1]]
 
         best = {}
         for a in range(2):
-            for q in range(4):
-                yb = psum.tile([P, 2, HALF], F32, name="yb", tag="bank%d" % (q + 4 * (1 - a)))
-                for c in range(2):
+            for q in range(QUARTERS):
+                yb = psum.tile([P, SIDES, HALF], F32, name="yb", tag="bank%d" % (q + QUARTERS * (1 - a)))
+                for c in range(SIDES):
                     nc.tensor.matmul_mx(
                         yb[:, c, :],
-                        lhsT=ew_d[q // 2][:, c, P * (q % 2):P * (q % 2 + 1)].bitcast(FP8X4), lhsT_scale=es_d[:, c, P * q:P * (q + 1)],
+                        lhsT=ew_d[q][:, c, :].bitcast(FP8X4), lhsT_scale=es_d[:, c, P * q:P * (q + 1)],
                         rhs=hc[a][:].bitcast(FP8X4), rhs_scale=hs[a][:],
                         start=True, stop=True,
                     )
@@ -182,20 +196,17 @@ def tile_picked_ycham_dens_p_kernel(
                 nc.vector.scalar_tensor_tensor(
                     best[a, q][:], yb[:, 1, :], neg_nb[:, 1, q:q + 1], best[a, q][:], ALU.add, ALU.max
                 )
+
         for n in range(S // P):
             tb = psum.tile([P, BANK], F32, name="tb", tag="bank%d" % n)
-            for q in range(4):
+            for q in range(QUARTERS):
                 nc.tensor.transpose(tb[:, P * q:P * (q + 1)], best[n // 2, q][:, P * (n % 2):P * (n % 2 + 1)], ident[:])
             rr = keep.tile([P, V], F32, name="rr%d" % n)
             res = keep.tile([P, V], F32, name="res%d" % n)
-            nc.vector.tensor_reduce(rr[:], tb[:].rearrange("p (v e) -> p v e", e=4), mybir.AxisListType.X, ALU.max)
-            if n < 3:
-                nc.scalar.activation(rr[:], rr[:], ACT.Relu, scale=-1.0, bias=own_t[:, n:n + 1])
-                nc.scalar.activation(rr[:], rr[:], ACT.Exp, scale=-1.0)
-            else:
-                nc.vector.tensor_scalar(rr[:], rr[:], own_t[:, n:n + 1], 0.0, ALU.subtract, ALU.min)
-                nc.scalar.activation(rr[:], rr[:], ACT.Exp)
-            if n < 2:
+            nc.vector.tensor_reduce(rr[:], tb[:].rearrange("p (v e) -> p v e", e=SIDE), mybir.AxisListType.X, ALU.max)
+            nc.scalar.activation(rr[:], rr[:], ACT.Relu, scale=-1.0, bias=own_t[:, n:n + 1])
+            nc.scalar.activation(rr[:], rr[:], ACT.Exp, scale=-1.0)
+            if n == 0:
                 nc.gpsimd.tensor_tensor(rr[:], rr[:], neg_cnt[:], ALU.mult)
                 nc.gpsimd.tensor_scalar(res[:], rr[:], 1.0, 1.0, ALU.mult, ALU.add)
             else:

@@ -28,7 +28,7 @@ SIDE = 4
 CNT_AT = 2048
 EW_B_AT = CNT_AT + 64 - 2048
 HS_AT = CNT_AT + 64
-ES_D_AT = HS_AT + 2 * HALF
+NB_AT = 4096
 
 
 def tile_picked_ycham_dens_p_kernel(
@@ -44,7 +44,7 @@ def tile_picked_ycham_dens_p_kernel(
         oth_t = keep.tile([P, U // 16], U16, name="oth_t")
         xs_tab = keep.tile([P, T], U8, name="xs_tab", align_bytes=64)
         es_tab = keep.tile([P, W], U8, name="es_tab", align_bytes=64)
-        nb_tab = keep.tile([P, W], F32, name="nb_tab", tag="nb_tab", align_bytes=64)
+        nb_tab = reuse.tile([P, W], F32, name="nb_tab", offset=NB_AT, align_bytes=64)
         xw_tab = [keep.tile([P, T], I32, name="xw_tab%d" % g, align_bytes=64) for g in range(PASSES)]
         ew_tab = keep.tile([P, W], I32, name="ew_tab", align_bytes=64)
         w_raw = [keep.tile([P, PACK, H], F32, name="w_raw%d" % g, tag="w_raw%d" % g, align_bytes=64) for g in range(PASSES)]
@@ -53,13 +53,15 @@ def tile_picked_ycham_dens_p_kernel(
         neg_cnt = keep.tile([P, V], F32, name="neg_cnt")
         ident = keep.tile([P, P], F32, name="ident", align_bytes=64)
         zero = keep.tile([P, 1], F32, name="zero")
+        es_d = keep.tile([P, SIDES, SIDE * V], U8, name="es_d", align_bytes=64)
         one = keep.tile([P, 1], F32, name="one")
 
         nc.vector.memset(es_tab[:].bitcast(I32), 0)
         nc.vector.memset(zero[:], 0.0)
-        nc.vector.memset(nb_tab[:].bitcast(I32), 0)
         nc.vector.memset(xs_tab[:].bitcast(I32), 0)
+        nc.vector.memset(nb_tab[:].bitcast(I32), 0)
         nc.vector.memset(ident[:], 0.0)
+        nc.vector.memset(es_d[:].bitcast(I32), 0)
         nc.scalar.activation(one[:], zero[:], ACT.Exp)
         make_identity(nc, ident[:], nomemset=True)
 
@@ -71,16 +73,13 @@ def tile_picked_ycham_dens_p_kernel(
 
         nc.sync.dma_start(oth_t[:], oth)
         nc.sync.dma_start(offs_t[:], offs)
-        for quad in range(4):
-            nc.sync.dma_start(
-                es_tab[32 * quad:32 * quad + 4, :].bitcast(I32), e_scales[0, 4 * quad:4 * quad + 4, :].bitcast(I32)
-            )
+        nc.sync.dma_start(es_tab[0:16, :].bitcast(I32), e_scales[0].bitcast(I32))
         load_w(0)
-        nc.sync.dma_start(nb_tab[0:1, :], nb[0:1, :])
         for quad in range(4):
             nc.sync.dma_start(
                 xs_tab[32 * quad:32 * quad + 8, :].bitcast(I32), x_scales[:, 4 * quad:4 * quad + 4, :].bitcast(I32)
             )
+        nc.sync.dma_start(nb_tab[0:1, :], nb[0:1, :])
         load_w(1)
         load_words(xw_tab[0], x_words[0])
         load_words(xw_tab[1], x_words[1])
@@ -105,16 +104,16 @@ def tile_picked_ycham_dens_p_kernel(
                     w_raw[g][:, :, 256 * half:256 * (half + 1)].rearrange("p j (m r) -> p m j r", r=PACK),
                 )
 
-        def quant_w(g, tag):
-            codes = keep.tile([P, H], U32, name="wc%d" % g, tag=tag, align_bytes=64)
+        def quant_w(g, codes):
             nc.vector.quantize_mx(codes[:].bitcast(FP8X4), ws[g][:], w_bf[g][:].rearrange("p r m j -> p (r m j)"))
             return codes
 
         nc.vector.tensor_copy(es[:], es_tab[:].indirect(oth_t[:]))
+        nc.vector.tensor_copy(xs[:], xs_tab[:].indirect(offs_t[:]))
         nc.vector.tensor_copy(nbg[:], nb_tab[:].indirect(oth_t[:]))
         cast_w(0)
         cast_w(1)
-        wc0 = quant_w(0, "nb_tab")
+        wc0 = quant_w(0, reuse.tile([P, H], U32, name="wc0", offset=NB_AT, align_bytes=64))
         warm = psum.tile([P, BANK], F32, name="warm", tag="bank4")
         for r in range(PACK):
             nc.tensor.matmul_mx(
@@ -123,9 +122,15 @@ def tile_picked_ycham_dens_p_kernel(
                 rhs=wc0[:].bitcast(FP8X4), rhs_scale=ws[0][:],
                 start=True, stop=True,
             )
-        nc.vector.tensor_copy(xs[:], xs_tab[:].indirect(offs_t[:]))
+        es_c = reuse.tile([P, SIDES, SIDE * V], U8, name="es_c", offset=NB_AT + 2048, align_bytes=64)
+        nc.vector.tensor_copy(es_c[:].bitcast(I32), es[:].bitcast(I32).rearrange("p (v c) -> p c v", c=SIDES))
+        for quad in range(4):
+            nc.sync.dma_start(
+                es_d[32 * quad:32 * quad + 4].rearrange("p c v -> p (c v)").bitcast(I32),
+                es_c[4 * quad:4 * quad + 4].rearrange("p c v -> p (c v)").bitcast(I32),
+            )
         nc.vector.tensor_copy(xw[0][:], xw_tab[0][:].bitcast(U32).indirect(offs_t[:]))
-        wc = [wc0, quant_w(1, "wc1")]
+        wc = [wc0, quant_w(1, keep.tile([P, H], U32, name="wc1", align_bytes=64))]
         for first, last in ((0, 1), (1, 2), (2, 4)):
             nc.vector.tensor_copy(
                 xw[1][:, P * first:P * last], xw_tab[1][:].bitcast(U32).indirect(offs_t[:, 8 * first:8 * last])
@@ -171,8 +176,6 @@ def tile_picked_ycham_dens_p_kernel(
         ew_a = keep.tile([P, SIDES, 2 * P], U32, name="ew_a", align_bytes=64)
         gather_ew(ew_a[:], 0, 2)
         nc.vector.tensor_scalar(neg_cnt[:], cnt_t[:, 0, :], -1.0, None, ALU.mult)
-        es_d = reuse.tile([P, SIDES, SIDE * V], U8, name="es_d", offset=ES_D_AT, align_bytes=64)
-        nc.vector.tensor_copy(es_d[:].bitcast(I32), es[:].bitcast(I32).rearrange("p (v c) -> p c v", c=SIDES))
         hs0 = quant_h(0)
         ew_b = reuse.tile([P, 2, SIDES, P], U32, name="ew_b", offset=EW_B_AT, align_bytes=64)
         for q in (2, 3):
@@ -197,19 +200,40 @@ def tile_picked_ycham_dens_p_kernel(
                     best[a, q][:], yb[:, 1, :], neg_nb[:, 1, q:q + 1], best[a, q][:], ALU.add, ALU.max
                 )
 
-        for n in range(S // P):
-            tb = psum.tile([P, BANK], F32, name="tb", tag="bank%d" % n)
+        def turn(n):
+            tb = psum.tile([P, BANK], F32, name="tb", tag="bank%d" % (QUARTERS + n if n else 0))
             for q in range(QUARTERS):
                 nc.tensor.transpose(tb[:, P * q:P * (q + 1)], best[n // 2, q][:, P * (n % 2):P * (n % 2 + 1)], ident[:])
-            rr = keep.tile([P, V], F32, name="rr%d" % n)
-            res = keep.tile([P, V], F32, name="res%d" % n)
-            nc.vector.tensor_reduce(rr[:], tb[:].rearrange("p (v e) -> p v e", e=SIDE), mybir.AxisListType.X, ALU.max)
-            nc.scalar.activation(rr[:], rr[:], ACT.Relu, scale=-1.0, bias=own_t[:, n:n + 1])
-            nc.scalar.activation(rr[:], rr[:], ACT.Exp, scale=-1.0)
-            if n == 0:
-                nc.gpsimd.tensor_tensor(rr[:], rr[:], neg_cnt[:], ALU.mult)
-                nc.gpsimd.tensor_scalar(res[:], rr[:], 1.0, 1.0, ALU.mult, ALU.add)
-            else:
-                nc.vector.tensor_tensor(rr[:], rr[:], neg_cnt[:], ALU.mult)
-                nc.vector.tensor_scalar(res[:], rr[:], one[:], None, ALU.add)
-            nc.sync.dma_start(out[P * n:P * (n + 1), :], res[:])
+            return tb
+
+        def largest(dst, src):
+            nc.vector.tensor_reduce(dst, src[:].rearrange("p (v e) -> p v e", e=SIDE), mybir.AxisListType.X, ALU.max)
+
+        def decay(dst, src, n):
+            nc.scalar.activation(dst, src, ACT.Relu, scale=-1.0, bias=own_t[:, n:n + 1])
+            nc.scalar.activation(dst, dst, ACT.Exp, scale=-1.0)
+
+        tb = [turn(n) for n in range(S // P)]
+        wide = reuse.tile([P, BANK], F32, name="wide", offset=EW_B_AT, align_bytes=64)
+        decay(wide[:], tb[1][:], 1)
+        rr0 = keep.tile([P, V], F32, name="rr0")
+        largest(rr0[:], tb[0])
+        decay(rr0[:], rr0[:], 0)
+        res0 = keep.tile([P, V], F32, name="res0")
+        nc.gpsimd.tensor_tensor(rr0[:], rr0[:], neg_cnt[:], ALU.mult)
+        nc.gpsimd.tensor_scalar(res0[:], rr0[:], 1.0, 1.0, ALU.mult, ALU.add)
+        nc.sync.dma_start(out[0:P, :], res0[:])
+        rr23 = keep.tile([P, 2, V], F32, name="rr23")
+        for i in range(2):
+            largest(rr23[:, i], tb[2 + i])
+            decay(rr23[:, i], rr23[:, i], 2 + i)
+        rr1 = keep.tile([P, V], F32, name="rr1", tag="best13", align_bytes=64)
+        largest(rr1[:], wide)
+        res23 = keep.tile([P, 2, V], F32, name="res23")
+        res1 = keep.tile([P, V], F32, name="res1")
+        nc.vector.tensor_tensor(rr23[:], rr23[:], neg_cnt[:].unsqueeze(1).to_broadcast([P, 2, V]), ALU.mult)
+        nc.vector.tensor_tensor(rr1[:], rr1[:], neg_cnt[:], ALU.mult)
+        nc.vector.tensor_scalar(res23[:], rr23[:], one[:], None, ALU.add)
+        nc.vector.tensor_scalar(res1[:], rr1[:], one[:], None, ALU.add)
+        nc.sync.dma_start(out[2 * P:4 * P, :].rearrange("(n p) v -> p n v", p=P), res23[:])
+        nc.sync.dma_start(out[P:2 * P, :], res1[:])

@@ -28,7 +28,7 @@ SIDE = 4
 CNT_AT = 2048
 EW_B_AT = CNT_AT + 64 - 2048
 HS_AT = CNT_AT + 64
-NB_AT = 4096
+ES_D_AT = HS_AT + 2 * HALF
 
 
 def tile_picked_ycham_dens_p_kernel(
@@ -44,7 +44,7 @@ def tile_picked_ycham_dens_p_kernel(
         oth_t = keep.tile([P, U // 16], U16, name="oth_t")
         xs_tab = keep.tile([P, T], U8, name="xs_tab", align_bytes=64)
         es_tab = keep.tile([P, W], U8, name="es_tab", align_bytes=64)
-        nb_tab = reuse.tile([P, W], F32, name="nb_tab", offset=NB_AT, align_bytes=64)
+        nb_tab = keep.tile([P, W], F32, name="nb_tab", tag="nb_tab", align_bytes=64)
         xw_tab = [keep.tile([P, T], I32, name="xw_tab%d" % g, align_bytes=64) for g in range(PASSES)]
         ew_tab = keep.tile([P, W], I32, name="ew_tab", align_bytes=64)
         w_raw = [keep.tile([P, PACK, H], F32, name="w_raw%d" % g, tag="w_raw%d" % g, align_bytes=64) for g in range(PASSES)]
@@ -53,15 +53,15 @@ def tile_picked_ycham_dens_p_kernel(
         neg_cnt = keep.tile([P, V], F32, name="neg_cnt")
         ident = keep.tile([P, P], F32, name="ident", align_bytes=64)
         zero = keep.tile([P, 1], F32, name="zero")
-        es_d = keep.tile([P, SIDES, SIDE * V], U8, name="es_d", align_bytes=64)
+        es = keep.tile([P, U], U8, name="es", align_bytes=64)
         one = keep.tile([P, 1], F32, name="one")
 
         nc.vector.memset(es_tab[:].bitcast(I32), 0)
         nc.vector.memset(zero[:], 0.0)
-        nc.vector.memset(xs_tab[:].bitcast(I32), 0)
         nc.vector.memset(nb_tab[:].bitcast(I32), 0)
+        nc.vector.memset(xs_tab[:].bitcast(I32), 0)
         nc.vector.memset(ident[:], 0.0)
-        nc.vector.memset(es_d[:].bitcast(I32), 0)
+        nc.vector.memset(es[:].bitcast(I32), 0)
         nc.scalar.activation(one[:], zero[:], ACT.Exp)
         make_identity(nc, ident[:], nomemset=True)
 
@@ -75,12 +75,16 @@ def tile_picked_ycham_dens_p_kernel(
         nc.sync.dma_start(offs_t[:], offs)
         nc.sync.dma_start(es_tab[0:16, :].bitcast(I32), e_scales[0].bitcast(I32))
         load_w(0)
+        nc.sync.dma_start(nb_tab[0:1, :], nb[0:1, :])
         for quad in range(4):
             nc.sync.dma_start(
                 xs_tab[32 * quad:32 * quad + 8, :].bitcast(I32), x_scales[:, 4 * quad:4 * quad + 4, :].bitcast(I32)
             )
-        nc.sync.dma_start(nb_tab[0:1, :], nb[0:1, :])
         load_w(1)
+        es_rows = keep.tile([P, U], U8, name="es_rows", align_bytes=64)
+        nc.vector.tensor_copy(es_rows[:], es_tab[:].indirect(oth_t[:]))
+        for quad in range(4):
+            nc.sync.dma_start(es[32 * quad:32 * quad + 4, :].bitcast(I32), es_rows[4 * quad:4 * quad + 4, :].bitcast(I32))
         load_words(xw_tab[0], x_words[0])
         load_words(xw_tab[1], x_words[1])
         load_words(ew_tab, e_words[0])
@@ -89,7 +93,6 @@ def tile_picked_ycham_dens_p_kernel(
             nc.sync.dma_start(own_t[:], own.rearrange("(n p) o -> p (n o)", p=P))
 
         xs = keep.tile([P, S], U8, name="xs", align_bytes=64)
-        es = keep.tile([P, U], U8, name="es", align_bytes=64)
         nbg = keep.tile([P, U], F32, name="nbg", align_bytes=64)
         xw = [keep.tile([P, S], U32, name="xw%d" % g, align_bytes=64) for g in range(PASSES)]
         w_bf = [keep.tile([P, PACK, P, PACK], BF16, name="w_bf%d" % g, align_bytes=64) for g in range(PASSES)]
@@ -104,16 +107,15 @@ def tile_picked_ycham_dens_p_kernel(
                     w_raw[g][:, :, 256 * half:256 * (half + 1)].rearrange("p j (m r) -> p m j r", r=PACK),
                 )
 
-        def quant_w(g, codes):
+        def quant_w(g, tag):
+            codes = keep.tile([P, H], U32, name="wc%d" % g, tag=tag, align_bytes=64)
             nc.vector.quantize_mx(codes[:].bitcast(FP8X4), ws[g][:], w_bf[g][:].rearrange("p r m j -> p (r m j)"))
             return codes
 
-        nc.vector.tensor_copy(es[:], es_tab[:].indirect(oth_t[:]))
-        nc.vector.tensor_copy(xs[:], xs_tab[:].indirect(offs_t[:]))
         nc.vector.tensor_copy(nbg[:], nb_tab[:].indirect(oth_t[:]))
         cast_w(0)
         cast_w(1)
-        wc0 = quant_w(0, reuse.tile([P, H], U32, name="wc0", offset=NB_AT, align_bytes=64))
+        wc0 = quant_w(0, "nb_tab")
         warm = psum.tile([P, BANK], F32, name="warm", tag="bank4")
         for r in range(PACK):
             nc.tensor.matmul_mx(
@@ -122,15 +124,9 @@ def tile_picked_ycham_dens_p_kernel(
                 rhs=wc0[:].bitcast(FP8X4), rhs_scale=ws[0][:],
                 start=True, stop=True,
             )
-        es_c = reuse.tile([P, SIDES, SIDE * V], U8, name="es_c", offset=NB_AT + 2048, align_bytes=64)
-        nc.vector.tensor_copy(es_c[:].bitcast(I32), es[:].bitcast(I32).rearrange("p (v c) -> p c v", c=SIDES))
-        for quad in range(4):
-            nc.sync.dma_start(
-                es_d[32 * quad:32 * quad + 4].rearrange("p c v -> p (c v)").bitcast(I32),
-                es_c[4 * quad:4 * quad + 4].rearrange("p c v -> p (c v)").bitcast(I32),
-            )
+        nc.vector.tensor_copy(xs[:], xs_tab[:].indirect(offs_t[:]))
         nc.vector.tensor_copy(xw[0][:], xw_tab[0][:].bitcast(U32).indirect(offs_t[:]))
-        wc = [wc0, quant_w(1, keep.tile([P, H], U32, name="wc1", align_bytes=64))]
+        wc = [wc0, quant_w(1, "wc1")]
         for first, last in ((0, 1), (1, 2), (2, 4)):
             nc.vector.tensor_copy(
                 xw[1][:, P * first:P * last], xw_tab[1][:].bitcast(U32).indirect(offs_t[:, 8 * first:8 * last])
@@ -176,6 +172,8 @@ def tile_picked_ycham_dens_p_kernel(
         ew_a = keep.tile([P, SIDES, 2 * P], U32, name="ew_a", align_bytes=64)
         gather_ew(ew_a[:], 0, 2)
         nc.vector.tensor_scalar(neg_cnt[:], cnt_t[:, 0, :], -1.0, None, ALU.mult)
+        es_d = reuse.tile([P, SIDES, SIDE * V], U8, name="es_d", offset=ES_D_AT, align_bytes=64)
+        nc.vector.tensor_copy(es_d[:].bitcast(I32), es[:].bitcast(I32).rearrange("p (v c) -> p c v", c=SIDES))
         hs0 = quant_h(0)
         ew_b = reuse.tile([P, 2, SIDES, P], U32, name="ew_b", offset=EW_B_AT, align_bytes=64)
         for q in (2, 3):

@@ -81,13 +81,13 @@ def tile_picked_ycham_dens_p_kernel(
                 xs_tab[32 * quad:32 * quad + 8, :].bitcast(I32), x_scales[:, 4 * quad:4 * quad + 4, :].bitcast(I32)
             )
         load_w(1)
+        load_words(xw_tab[0], x_words[0])
+        load_words(xw_tab[1], x_words[1])
+        load_words(ew_tab, e_words[0])
         es_rows = keep.tile([P, U], U8, name="es_rows", align_bytes=64)
         nc.vector.tensor_copy(es_rows[:], es_tab[:].indirect(oth_t[:]))
         for quad in range(4):
             nc.sync.dma_start(es[32 * quad:32 * quad + 4, :].bitcast(I32), es_rows[4 * quad:4 * quad + 4, :].bitcast(I32))
-        load_words(xw_tab[0], x_words[0])
-        load_words(xw_tab[1], x_words[1])
-        load_words(ew_tab, e_words[0])
         nc.sync.dma_start(cnt_t[:, 0, :], cnt)
         with nc.allow_non_contiguous_dma(reason="one value a partition and token block"):
             nc.sync.dma_start(own_t[:], own.rearrange("(n p) o -> p (n o)", p=P))
@@ -198,40 +198,19 @@ def tile_picked_ycham_dens_p_kernel(
                     best[a, q][:], yb[:, 1, :], neg_nb[:, 1, q:q + 1], best[a, q][:], ALU.add, ALU.max
                 )
 
-        def turn(n):
-            tb = psum.tile([P, BANK], F32, name="tb", tag="bank%d" % (QUARTERS + n if n else 0))
+        for n in range(S // P):
+            tb = psum.tile([P, BANK], F32, name="tb", tag="bank%d" % n)
             for q in range(QUARTERS):
                 nc.tensor.transpose(tb[:, P * q:P * (q + 1)], best[n // 2, q][:, P * (n % 2):P * (n % 2 + 1)], ident[:])
-            return tb
-
-        def largest(dst, src):
-            nc.vector.tensor_reduce(dst, src[:].rearrange("p (v e) -> p v e", e=SIDE), mybir.AxisListType.X, ALU.max)
-
-        def decay(dst, src, n):
-            nc.scalar.activation(dst, src, ACT.Relu, scale=-1.0, bias=own_t[:, n:n + 1])
-            nc.scalar.activation(dst, dst, ACT.Exp, scale=-1.0)
-
-        tb = [turn(n) for n in range(S // P)]
-        wide = reuse.tile([P, BANK], F32, name="wide", offset=EW_B_AT, align_bytes=64)
-        decay(wide[:], tb[1][:], 1)
-        rr0 = keep.tile([P, V], F32, name="rr0")
-        largest(rr0[:], tb[0])
-        decay(rr0[:], rr0[:], 0)
-        res0 = keep.tile([P, V], F32, name="res0")
-        nc.gpsimd.tensor_tensor(rr0[:], rr0[:], neg_cnt[:], ALU.mult)
-        nc.gpsimd.tensor_scalar(res0[:], rr0[:], 1.0, 1.0, ALU.mult, ALU.add)
-        nc.sync.dma_start(out[0:P, :], res0[:])
-        rr23 = keep.tile([P, 2, V], F32, name="rr23")
-        for i in range(2):
-            largest(rr23[:, i], tb[2 + i])
-            decay(rr23[:, i], rr23[:, i], 2 + i)
-        rr1 = keep.tile([P, V], F32, name="rr1", tag="best13", align_bytes=64)
-        largest(rr1[:], wide)
-        res23 = keep.tile([P, 2, V], F32, name="res23")
-        res1 = keep.tile([P, V], F32, name="res1")
-        nc.vector.tensor_tensor(rr23[:], rr23[:], neg_cnt[:].unsqueeze(1).to_broadcast([P, 2, V]), ALU.mult)
-        nc.vector.tensor_tensor(rr1[:], rr1[:], neg_cnt[:], ALU.mult)
-        nc.vector.tensor_scalar(res23[:], rr23[:], one[:], None, ALU.add)
-        nc.vector.tensor_scalar(res1[:], rr1[:], one[:], None, ALU.add)
-        nc.sync.dma_start(out[2 * P:4 * P, :].rearrange("(n p) v -> p n v", p=P), res23[:])
-        nc.sync.dma_start(out[P:2 * P, :], res1[:])
+            rr = keep.tile([P, V], F32, name="rr%d" % n)
+            res = keep.tile([P, V], F32, name="res%d" % n)
+            nc.vector.tensor_reduce(rr[:], tb[:].rearrange("p (v e) -> p v e", e=SIDE), mybir.AxisListType.X, ALU.max)
+            nc.scalar.activation(rr[:], rr[:], ACT.Relu, scale=-1.0, bias=own_t[:, n:n + 1])
+            nc.scalar.activation(rr[:], rr[:], ACT.Exp, scale=-1.0)
+            if n == 0:
+                nc.gpsimd.tensor_tensor(rr[:], rr[:], neg_cnt[:], ALU.mult)
+                nc.gpsimd.tensor_scalar(res[:], rr[:], 1.0, 1.0, ALU.mult, ALU.add)
+            else:
+                nc.vector.tensor_tensor(rr[:], rr[:], neg_cnt[:], ALU.mult)
+                nc.vector.tensor_scalar(res[:], rr[:], one[:], None, ALU.add)
+            nc.sync.dma_start(out[P * n:P * (n + 1), :], res[:])

@@ -49,8 +49,7 @@ def tile_picked_ycham_dens_p_kernel(
         ew_tab = keep.tile([P, W], I32, name="ew_tab", align_bytes=64)
         w_raw = [keep.tile([P, PACK, H], F32, name="w_raw%d" % g, tag="w_raw%d" % g, align_bytes=64) for g in range(PASSES)]
         own_t = keep.tile([P, S // P], F32, name="own_t")
-        cnt_t = reuse.tile([P, 2, V], F32, name="cnt_t", offset=CNT_AT, align_bytes=64)
-        neg_cnt = keep.tile([P, V], F32, name="neg_cnt")
+        cnt_t = keep.tile([P, V], F32, name="cnt_t")
         ident = keep.tile([P, P], F32, name="ident", align_bytes=64)
         zero = keep.tile([P, 1], F32, name="zero")
         es = keep.tile([P, U], U8, name="es", align_bytes=64)
@@ -75,7 +74,7 @@ def tile_picked_ycham_dens_p_kernel(
         nc.sync.dma_start(offs_t[:], offs)
         nc.sync.dma_start(es_tab[0:16, :].bitcast(I32), e_scales[0].bitcast(I32))
         load_w(0)
-        nc.sync.dma_start(nb_tab[0:1, :], nb[0:1, :])
+        nc.scalar.dma_start(nb_tab[0:1, :], nb[0:1, :])
         for quad in range(4):
             nc.sync.dma_start(
                 xs_tab[32 * quad:32 * quad + 8, :].bitcast(I32), x_scales[:, 4 * quad:4 * quad + 4, :].bitcast(I32)
@@ -84,11 +83,11 @@ def tile_picked_ycham_dens_p_kernel(
         load_words(xw_tab[0], x_words[0])
         load_words(xw_tab[1], x_words[1])
         load_words(ew_tab, e_words[0])
-        es_rows = keep.tile([P, U], U8, name="es_rows", align_bytes=64)
+        es_rows = reuse.tile([P, U], U8, name="es_rows", offset=CNT_AT, align_bytes=64)
         nc.vector.tensor_copy(es_rows[:], es_tab[:].indirect(oth_t[:]))
         for quad in range(4):
             nc.sync.dma_start(es[32 * quad:32 * quad + 4, :].bitcast(I32), es_rows[4 * quad:4 * quad + 4, :].bitcast(I32))
-        nc.sync.dma_start(cnt_t[:, 0, :], cnt)
+        nc.sync.dma_start(cnt_t[:], cnt)
         with nc.allow_non_contiguous_dma(reason="one value a partition and token block"):
             nc.sync.dma_start(own_t[:], own.rearrange("(n p) o -> p (n o)", p=P))
 
@@ -115,7 +114,7 @@ def tile_picked_ycham_dens_p_kernel(
         nc.vector.tensor_copy(nbg[:], nb_tab[:].indirect(oth_t[:]))
         cast_w(0)
         cast_w(1)
-        wc0 = quant_w(0, "nb_tab")
+        wc0 = quant_w(0, "wc0")
         warm = psum.tile([P, BANK], F32, name="warm", tag="bank4")
         for r in range(PACK):
             nc.tensor.matmul_mx(
@@ -171,8 +170,7 @@ def tile_picked_ycham_dens_p_kernel(
 
         ew_a = keep.tile([P, SIDES, 2 * P], U32, name="ew_a", align_bytes=64)
         gather_ew(ew_a[:], 0, 2)
-        nc.vector.tensor_scalar(neg_cnt[:], cnt_t[:, 0, :], -1.0, None, ALU.mult)
-        es_d = reuse.tile([P, SIDES, SIDE * V], U8, name="es_d", offset=ES_D_AT, align_bytes=64)
+        es_d = keep.tile([P, SIDES, SIDE * V], U8, name="es_d", align_bytes=64)
         nc.vector.tensor_copy(es_d[:].bitcast(I32), es[:].bitcast(I32).rearrange("p (v c) -> p c v", c=SIDES))
         hs0 = quant_h(0)
         ew_b = reuse.tile([P, 2, SIDES, P], U32, name="ew_b", offset=EW_B_AT, align_bytes=64)
@@ -198,19 +196,40 @@ def tile_picked_ycham_dens_p_kernel(
                     best[a, q][:], yb[:, 1, :], neg_nb[:, 1, q:q + 1], best[a, q][:], ALU.add, ALU.max
                 )
 
-        for n in range(S // P):
-            tb = psum.tile([P, BANK], F32, name="tb", tag="bank%d" % n)
+        def turn(n):
+            tb = psum.tile([P, BANK], F32, name="tb", tag="bank%d" % (QUARTERS + n if n else 0))
             for q in range(QUARTERS):
                 nc.tensor.transpose(tb[:, P * q:P * (q + 1)], best[n // 2, q][:, P * (n % 2):P * (n % 2 + 1)], ident[:])
-            rr = keep.tile([P, V], F32, name="rr%d" % n)
-            res = keep.tile([P, V], F32, name="res%d" % n)
-            nc.vector.tensor_reduce(rr[:], tb[:].rearrange("p (v e) -> p v e", e=SIDE), mybir.AxisListType.X, ALU.max)
-            nc.scalar.activation(rr[:], rr[:], ACT.Relu, scale=-1.0, bias=own_t[:, n:n + 1])
-            nc.scalar.activation(rr[:], rr[:], ACT.Exp, scale=-1.0)
-            if n == 0:
-                nc.gpsimd.tensor_tensor(rr[:], rr[:], neg_cnt[:], ALU.mult)
-                nc.gpsimd.tensor_scalar(res[:], rr[:], 1.0, 1.0, ALU.mult, ALU.add)
-            else:
-                nc.vector.tensor_tensor(rr[:], rr[:], neg_cnt[:], ALU.mult)
-                nc.vector.tensor_scalar(res[:], rr[:], one[:], None, ALU.add)
-            nc.sync.dma_start(out[P * n:P * (n + 1), :], res[:])
+            return tb
+
+        def largest(dst, src):
+            nc.vector.tensor_reduce(dst, src[:].rearrange("p (v e) -> p v e", e=SIDE), mybir.AxisListType.X, ALU.max)
+
+        def decay(dst, src, n):
+            nc.scalar.activation(dst, src, ACT.Relu, scale=-1.0, bias=own_t[:, n:n + 1])
+            nc.scalar.activation(dst, dst, ACT.Exp, scale=-1.0)
+
+        tb = [turn(n) for n in range(S // P)]
+        wide = reuse.tile([P, BANK], F32, name="wide", offset=EW_B_AT, align_bytes=64)
+        decay(wide[:], tb[1][:], 1)
+        rr0 = keep.tile([P, V], F32, name="rr0")
+        largest(rr0[:], tb[0])
+        decay(rr0[:], rr0[:], 0)
+        res0 = keep.tile([P, V], F32, name="res0")
+        nc.gpsimd.tensor_tensor(rr0[:], rr0[:], cnt_t[:], ALU.mult)
+        nc.gpsimd.tensor_scalar(res0[:], rr0[:], -1.0, 1.0, ALU.mult, ALU.add)
+        nc.sync.dma_start(out[0:P, :], res0[:])
+        rr23 = keep.tile([P, 2, V], F32, name="rr23")
+        for i in range(2):
+            largest(rr23[:, i], tb[2 + i])
+            decay(rr23[:, i], rr23[:, i], 2 + i)
+        rr1 = keep.tile([P, V], F32, name="rr1", tag="best13", align_bytes=64)
+        largest(rr1[:], wide)
+        res23 = keep.tile([P, 2, V], F32, name="res23")
+        res1 = keep.tile([P, V], F32, name="res1")
+        nc.vector.tensor_tensor(rr23[:], rr23[:], cnt_t[:].unsqueeze(1).to_broadcast([P, 2, V]), ALU.mult)
+        nc.vector.tensor_tensor(rr1[:], rr1[:], cnt_t[:], ALU.mult)
+        nc.vector.tensor_scalar(res23[:], rr23[:], -1.0, one[:], ALU.mult, ALU.add)
+        nc.vector.tensor_scalar(res1[:], rr1[:], -1.0, one[:], ALU.mult, ALU.add)
+        nc.sync.dma_start(out[2 * P:4 * P, :].rearrange("(n p) v -> p n v", p=P), res23[:])
+        nc.sync.dma_start(out[P:2 * P, :], res1[:])

@@ -141,17 +141,25 @@ def tile_picked_ycham_dens_p_kernel(
         neg_nb = keep.tile([P, SIDES, QUARTERS], F32, name="neg_nb", align_bytes=64)
         nc.sync.dma_start(neg_nb[:].rearrange("p c q -> p (c q)"), nb_row[:].rearrange("o m c q -> o m (c q)"))
 
+        def first_product(hb, n, g, r, start, stop):
+            cols = slice(P * n, P * (n + 1))
+            nc.tensor.matmul_mx(
+                hb[:, P * r:P * (r + 1)],
+                lhsT=wc[g][:, P * r:P * (r + 1)].bitcast(FP8X4), lhsT_scale=ws[g][:, P * r:P * (r + 1)],
+                rhs=xw[g][:, cols].bitcast(FP8X4), rhs_scale=xs[4 * g:P, cols],
+                start=start, stop=stop,
+            )
+
         for n in range(S // P):
             hb = psum.tile([P, BANK], F32, name="hb", tag="bank%d" % n)
-            cols = slice(P * n, P * (n + 1))
-            for r in range(PACK):
+            if n < 2:
                 for g in range(PASSES):
-                    nc.tensor.matmul_mx(
-                        hb[:, P * r:P * (r + 1)],
-                        lhsT=wc[g][:, P * r:P * (r + 1)].bitcast(FP8X4), lhsT_scale=ws[g][:, P * r:P * (r + 1)],
-                        rhs=xw[g][:, cols].bitcast(FP8X4), rhs_scale=xs[4 * g:P, cols],
-                        start=(g == 0), stop=(g == PASSES - 1),
-                    )
+                    for r in range(PACK):
+                        first_product(hb, n, g, r, (g, r) == (0, 0), (g, r) == (PASSES - 1, PACK - 1))
+            else:
+                for r in range(PACK):
+                    for g in range(PASSES):
+                        first_product(hb, n, g, r, g == 0, g == PASSES - 1)
             nc.scalar.copy(
                 h_bf[n // 2][:, P * (n % 2):P * (n % 2 + 1), :],
                 hb[:].rearrange("p (r t) -> p t r", r=PACK),

@@ -56,8 +56,8 @@ def tile_picked_ycham_dens_p_kernel(
         one = keep.tile([P, 1], F32, name="one")
 
         nc.vector.memset(es_tab[:].bitcast(I32), 0)
-        nc.vector.memset(zero[:], 0.0)
         nc.vector.memset(nb_tab[:].bitcast(I32), 0)
+        nc.vector.memset(zero[:], 0.0)
         nc.vector.memset(xs_tab[:].bitcast(I32), 0)
         nc.vector.memset(ident[:], 0.0)
         nc.vector.memset(es[:].bitcast(I32), 0)
@@ -116,7 +116,7 @@ def tile_picked_ycham_dens_p_kernel(
         cast_w(1)
         wc0 = quant_w(0, "wc0")
         warm = psum.tile([P, BANK], F32, name="warm", tag="bank4")
-        for r in range(PACK):
+        for r in range(2):
             nc.tensor.matmul_mx(
                 warm[:],
                 lhsT=wc0[:, P * r:P * (r + 1)].bitcast(FP8X4), lhsT_scale=ws[0][:, P * r:P * (r + 1)],

@@ -47,12 +47,15 @@ def tile_picked_ycham_dens_p_kernel(
         nb_tab = keep.tile([P, W], F32, name="nb_tab", tag="nb_tab", align_bytes=64)
         xw_tab = [keep.tile([P, T], I32, name="xw_tab%d" % g, align_bytes=64) for g in range(PASSES)]
         ew_tab = keep.tile([P, W], I32, name="ew_tab", align_bytes=64)
-        w_raw = [keep.tile([P, PACK, H], F32, name="w_raw%d" % g, tag="w_raw%d" % g, align_bytes=64) for g in range(PASSES)]
+        w_raw = [
+            reuse.tile([P, PACK, H], F32, name="w_raw0", offset=0, align_bytes=64),
+            keep.tile([P, PACK, H], F32, name="w_raw1", tag="w_raw1", align_bytes=64),
+        ]
         own_t = keep.tile([P, S // P], F32, name="own_t")
         cnt_t = keep.tile([P, V], F32, name="cnt_t")
         ident = keep.tile([P, P], F32, name="ident", align_bytes=64)
         zero = keep.tile([P, 1], F32, name="zero")
-        es = keep.tile([P, U], U8, name="es", align_bytes=64)
+        es_d = keep.tile([P, SIDES, SIDE * V], U8, name="es_d", align_bytes=64)
         one = keep.tile([P, 1], F32, name="one")
 
         nc.vector.memset(es_tab[:].bitcast(I32), 0)
@@ -60,7 +63,7 @@ def tile_picked_ycham_dens_p_kernel(
         nc.vector.memset(zero[:], 0.0)
         nc.vector.memset(xs_tab[:].bitcast(I32), 0)
         nc.vector.memset(ident[:], 0.0)
-        nc.vector.memset(es[:].bitcast(I32), 0)
+        nc.vector.memset(es_d[:].bitcast(I32), 0)
         nc.scalar.activation(one[:], zero[:], ACT.Exp)
         make_identity(nc, ident[:], nomemset=True)
 
@@ -83,14 +86,9 @@ def tile_picked_ycham_dens_p_kernel(
         load_words(xw_tab[0], x_words[0])
         load_words(xw_tab[1], x_words[1])
         load_words(ew_tab, e_words[0])
-        es_rows = reuse.tile([P, U], U8, name="es_rows", offset=CNT_AT, align_bytes=64)
-        nc.vector.tensor_copy(es_rows[:], es_tab[:].indirect(oth_t[:]))
-        for quad in range(4):
-            nc.sync.dma_start(es[32 * quad:32 * quad + 4, :].bitcast(I32), es_rows[4 * quad:4 * quad + 4, :].bitcast(I32))
-        nc.sync.dma_start(cnt_t[:], cnt)
-        with nc.allow_non_contiguous_dma(reason="one value a partition and token block"):
-            nc.sync.dma_start(own_t[:], own.rearrange("(n p) o -> p (n o)", p=P))
 
+        es_rows = keep.tile([P, U], U8, name="es_rows", align_bytes=64)
+        nc.vector.tensor_copy(es_rows[:], es_tab[:].indirect(oth_t[:]))
         xs = keep.tile([P, S], U8, name="xs", align_bytes=64)
         nbg = keep.tile([P, U], F32, name="nbg", align_bytes=64)
         xw = [keep.tile([P, S], U32, name="xw%d" % g, align_bytes=64) for g in range(PASSES)]
@@ -115,6 +113,16 @@ def tile_picked_ycham_dens_p_kernel(
         cast_w(0)
         cast_w(1)
         wc0 = quant_w(0, "wc0")
+        es_c = reuse.tile([P, SIDES, SIDE * V], U8, name="es_c", offset=CNT_AT, align_bytes=64)
+        nc.vector.tensor_copy(es_c[:].bitcast(I32), es_rows[:].bitcast(I32).rearrange("p (v c) -> p c v", c=SIDES))
+        for quad in range(4):
+            nc.sync.dma_start(
+                es_d[32 * quad:32 * quad + 4].rearrange("p c v -> p (c v)").bitcast(I32),
+                es_c[4 * quad:4 * quad + 4].rearrange("p c v -> p (c v)").bitcast(I32),
+            )
+        nc.sync.dma_start(cnt_t[:], cnt)
+        with nc.allow_non_contiguous_dma(reason="one value a partition and token block"):
+            nc.sync.dma_start(own_t[:], own.rearrange("(n p) o -> p (n o)", p=P))
         warm = psum.tile([P, BANK], F32, name="warm", tag="bank4")
         for r in range(2):
             nc.tensor.matmul_mx(
@@ -178,8 +186,6 @@ def tile_picked_ycham_dens_p_kernel(
 
         ew_a = keep.tile([P, SIDES, 2 * P], U32, name="ew_a", align_bytes=64)
         gather_ew(ew_a[:], 0, 2)
-        es_d = keep.tile([P, SIDES, SIDE * V], U8, name="es_d", align_bytes=64)
-        nc.vector.tensor_copy(es_d[:].bitcast(I32), es[:].bitcast(I32).rearrange("p (v c) -> p c v", c=SIDES))
         hs0 = quant_h(0)
         ew_b = reuse.tile([P, 2, SIDES, P], U32, name="ew_b", offset=EW_B_AT, align_bytes=64)
         for q in (2, 3):

@@ -60,8 +60,8 @@ def tile_picked_ycham_dens_p_kernel(
 
         nc.vector.memset(es_tab[:].bitcast(I32), 0)
         nc.vector.memset(nb_tab[:].bitcast(I32), 0)
-        nc.vector.memset(zero[:], 0.0)
         nc.vector.memset(xs_tab[:].bitcast(I32), 0)
+        nc.vector.memset(zero[:], 0.0)
         nc.vector.memset(ident[:], 0.0)
         nc.vector.memset(es_d[:].bitcast(I32), 0)
         nc.scalar.activation(one[:], zero[:], ACT.Exp)
@@ -75,12 +75,12 @@ def tile_picked_ycham_dens_p_kernel(
 
         nc.sync.dma_start(oth_t[:], oth)
         nc.sync.dma_start(offs_t[:], offs)
-        nc.sync.dma_start(es_tab[0:16, :].bitcast(I32), e_scales[0].bitcast(I32))
+        nc.sync.dma_start(es_tab[16:32, :].bitcast(I32), e_scales[0].bitcast(I32))
         load_w(0)
         nc.scalar.dma_start(nb_tab[0:1, :], nb[0:1, :])
         for quad in range(4):
             nc.sync.dma_start(
-                xs_tab[32 * quad:32 * quad + 8, :].bitcast(I32), x_scales[:, 4 * quad:4 * quad + 4, :].bitcast(I32)
+                xs_tab[32 * quad + 4:32 * quad + 12, :].bitcast(I32), x_scales[:, 4 * quad:4 * quad + 4, :].bitcast(I32)
             )
         load_w(1)
         load_words(xw_tab[0], x_words[0])
@@ -118,7 +118,7 @@ def tile_picked_ycham_dens_p_kernel(
         for quad in range(4):
             nc.sync.dma_start(
                 es_d[32 * quad:32 * quad + 4].rearrange("p c v -> p (c v)").bitcast(I32),
-                es_c[4 * quad:4 * quad + 4].rearrange("p c v -> p (c v)").bitcast(I32),
+                es_c[16 + 4 * quad:16 + 4 * quad + 4].rearrange("p c v -> p (c v)").bitcast(I32),
             )
         nc.sync.dma_start(cnt_t[:], cnt)
         with nc.allow_non_contiguous_dma(reason="one value a partition and token block"):
@@ -154,7 +154,7 @@ def tile_picked_ycham_dens_p_kernel(
             nc.tensor.matmul_mx(
                 hb[:, P * r:P * (r + 1)],
                 lhsT=wc[g][:, P * r:P * (r + 1)].bitcast(FP8X4), lhsT_scale=ws[g][:, P * r:P * (r + 1)],
-                rhs=xw[g][:, cols].bitcast(FP8X4), rhs_scale=xs[4 * g:P, cols],
+                rhs=xw[g][:, cols].bitcast(FP8X4), rhs_scale=xs[4 * g + 4:P, cols],
                 start=start, stop=stop,
             )
 

@@ -25,10 +25,13 @@ QUARTERS = 4
 SIDES = 2
 SIDE = 4
 
-CNT_AT = 2048
-EW_B_AT = CNT_AT + 64 - 2048
-HS_AT = CNT_AT + 64
-ES_D_AT = HS_AT + 2 * HALF
+XS_FROM = 4
+ES_FROM = 16
+WARM_UPS = 2
+
+ES_C_AT = 2048
+EW_B_AT = ES_C_AT + 64 - 2048
+HS_AT = ES_C_AT + 64
 
 
 def tile_picked_ycham_dens_p_kernel(
@@ -44,12 +47,12 @@ def tile_picked_ycham_dens_p_kernel(
         oth_t = keep.tile([P, U // 16], U16, name="oth_t")
         xs_tab = keep.tile([P, T], U8, name="xs_tab", align_bytes=64)
         es_tab = keep.tile([P, W], U8, name="es_tab", align_bytes=64)
-        nb_tab = keep.tile([P, W], F32, name="nb_tab", tag="nb_tab", align_bytes=64)
+        nb_tab = keep.tile([P, W], F32, name="nb_tab", align_bytes=64)
         xw_tab = [keep.tile([P, T], I32, name="xw_tab%d" % g, align_bytes=64) for g in range(PASSES)]
         ew_tab = keep.tile([P, W], I32, name="ew_tab", align_bytes=64)
         w_raw = [
             reuse.tile([P, PACK, H], F32, name="w_raw0", offset=0, align_bytes=64),
-            keep.tile([P, PACK, H], F32, name="w_raw1", tag="w_raw1", align_bytes=64),
+            keep.tile([P, PACK, H], F32, name="w_raw1", align_bytes=64),
         ]
         own_t = keep.tile([P, S // P], F32, name="own_t")
         cnt_t = keep.tile([P, V], F32, name="cnt_t")
@@ -75,13 +78,12 @@ def tile_picked_ycham_dens_p_kernel(
 
         nc.sync.dma_start(oth_t[:], oth)
         nc.sync.dma_start(offs_t[:], offs)
-        nc.sync.dma_start(es_tab[16:32, :].bitcast(I32), e_scales[0].bitcast(I32))
+        nc.sync.dma_start(es_tab[ES_FROM:ES_FROM + 16, :].bitcast(I32), e_scales[0].bitcast(I32))
         load_w(0)
         nc.scalar.dma_start(nb_tab[0:1, :], nb[0:1, :])
         for quad in range(4):
-            nc.sync.dma_start(
-                xs_tab[32 * quad + 4:32 * quad + 12, :].bitcast(I32), x_scales[:, 4 * quad:4 * quad + 4, :].bitcast(I32)
-            )
+            rows = slice(32 * quad + XS_FROM, 32 * quad + XS_FROM + 4 * PASSES)
+            nc.sync.dma_start(xs_tab[rows, :].bitcast(I32), x_scales[:, 4 * quad:4 * quad + 4, :].bitcast(I32))
         load_w(1)
         load_words(xw_tab[0], x_words[0])
         load_words(xw_tab[1], x_words[1])
@@ -97,43 +99,47 @@ def tile_picked_ycham_dens_p_kernel(
         h_bf = [keep.tile([P, HALF, PACK], BF16, name="h_bf%d" % a, align_bytes=64) for a in range(2)]
         hc = [keep.tile([P, HALF], U32, name="hc%d" % a, align_bytes=64) for a in range(2)]
 
+        wc = [keep.tile([P, H], U32, name="wc%d" % g, align_bytes=64) for g in range(PASSES)]
+
         def cast_w(g):
-            for half in range(2):
+            for r in (0, 2):
                 nc.scalar.copy(
-                    w_bf[g][:, :, 64 * half:64 * (half + 1), :].rearrange("p r m j -> p m j r"),
-                    w_raw[g][:, :, 256 * half:256 * (half + 1)].rearrange("p j (m r) -> p m j r", r=PACK),
+                    w_bf[g][:, r:r + 2].rearrange("p r m j -> p m j r"),
+                    w_raw[g][:].rearrange("p j (m r) -> p m j r", r=PACK)[:, :, :, r:r + 2],
                 )
 
-        def quant_w(g, tag):
-            codes = keep.tile([P, H], U32, name="wc%d" % g, tag=tag, align_bytes=64)
-            nc.vector.quantize_mx(codes[:].bitcast(FP8X4), ws[g][:], w_bf[g][:].rearrange("p r m j -> p (r m j)"))
-            return codes
+        def quant_w(g, first, last):
+            cols = slice(P * first, P * last)
+            nc.vector.quantize_mx(
+                wc[g][:, cols].bitcast(FP8X4), ws[g][:, cols], w_bf[g][:, first:last].rearrange("p r m j -> p (r m j)")
+            )
 
         nc.vector.tensor_copy(nbg[:], nb_tab[:].indirect(oth_t[:]))
         cast_w(0)
         cast_w(1)
-        wc0 = quant_w(0, "wc0")
-        es_c = reuse.tile([P, SIDES, SIDE * V], U8, name="es_c", offset=CNT_AT, align_bytes=64)
+        quant_w(0, 0, 4)
+        es_c = reuse.tile([P, SIDES, SIDE * V], U8, name="es_c", offset=ES_C_AT, align_bytes=64)
         nc.vector.tensor_copy(es_c[:].bitcast(I32), es_rows[:].bitcast(I32).rearrange("p (v c) -> p c v", c=SIDES))
         for quad in range(4):
             nc.sync.dma_start(
                 es_d[32 * quad:32 * quad + 4].rearrange("p c v -> p (c v)").bitcast(I32),
-                es_c[16 + 4 * quad:16 + 4 * quad + 4].rearrange("p c v -> p (c v)").bitcast(I32),
+                es_c[ES_FROM + 4 * quad:ES_FROM + 4 * quad + 4].rearrange("p c v -> p (c v)").bitcast(I32),
             )
         nc.sync.dma_start(cnt_t[:], cnt)
         with nc.allow_non_contiguous_dma(reason="one value a partition and token block"):
             nc.sync.dma_start(own_t[:], own.rearrange("(n p) o -> p (n o)", p=P))
         warm = psum.tile([P, BANK], F32, name="warm", tag="bank4")
-        for r in range(2):
+        for r in range(WARM_UPS):
             nc.tensor.matmul_mx(
                 warm[:],
-                lhsT=wc0[:, P * r:P * (r + 1)].bitcast(FP8X4), lhsT_scale=ws[0][:, P * r:P * (r + 1)],
-                rhs=wc0[:].bitcast(FP8X4), rhs_scale=ws[0][:],
+                lhsT=wc[0][:, P * r:P * (r + 1)].bitcast(FP8X4), lhsT_scale=ws[0][:, P * r:P * (r + 1)],
+                rhs=wc[0][:].bitcast(FP8X4), rhs_scale=ws[0][:],
                 start=True, stop=True,
             )
         nc.vector.tensor_copy(xs[:], xs_tab[:].indirect(offs_t[:]))
+        quant_w(1, 0, 2)
         nc.vector.tensor_copy(xw[0][:], xw_tab[0][:].bitcast(U32).indirect(offs_t[:]))
-        wc = [wc0, quant_w(1, "wc1")]
+        quant_w(1, 2, 4)
         for first, last in ((0, 1), (1, 2), (2, 4)):
             nc.vector.tensor_copy(
                 xw[1][:, P * first:P * last], xw_tab[1][:].bitcast(U32).indirect(offs_t[:, 8 * first:8 * last])
@@ -154,13 +160,13 @@ def tile_picked_ycham_dens_p_kernel(
             nc.tensor.matmul_mx(
                 hb[:, P * r:P * (r + 1)],
                 lhsT=wc[g][:, P * r:P * (r + 1)].bitcast(FP8X4), lhsT_scale=ws[g][:, P * r:P * (r + 1)],
-                rhs=xw[g][:, cols].bitcast(FP8X4), rhs_scale=xs[4 * g + 4:P, cols],
+                rhs=xw[g][:, cols].bitcast(FP8X4), rhs_scale=xs[XS_FROM + 4 * g:P, cols],
                 start=start, stop=stop,
             )
 
         for n in range(S // P):
             hb = psum.tile([P, BANK], F32, name="hb", tag="bank%d" % n)
-            if n < 2:
+            if n < HALF // P:
                 for g in range(PASSES):
                     for r in range(PACK):
                         first_product(hb, n, g, r, (g, r) == (0, 0), (g, r) == (PASSES - 1, PACK - 1))
@@ -226,24 +232,19 @@ def tile_picked_ycham_dens_p_kernel(
         tb = [turn(n) for n in range(S // P)]
         wide = reuse.tile([P, BANK], F32, name="wide", offset=EW_B_AT, align_bytes=64)
         decay(wide[:], tb[1][:], 1)
-        rr0 = keep.tile([P, V], F32, name="rr0")
-        largest(rr0[:], tb[0])
-        decay(rr0[:], rr0[:], 0)
-        res0 = keep.tile([P, V], F32, name="res0")
-        nc.gpsimd.tensor_tensor(rr0[:], rr0[:], cnt_t[:], ALU.mult)
-        nc.gpsimd.tensor_scalar(res0[:], rr0[:], -1.0, 1.0, ALU.mult, ALU.add)
-        nc.sync.dma_start(out[0:P, :], res0[:])
-        rr23 = keep.tile([P, 2, V], F32, name="rr23")
-        for i in range(2):
-            largest(rr23[:, i], tb[2 + i])
-            decay(rr23[:, i], rr23[:, i], 2 + i)
-        rr1 = keep.tile([P, V], F32, name="rr1", tag="best13", align_bytes=64)
-        largest(rr1[:], wide)
-        res23 = keep.tile([P, 2, V], F32, name="res23")
-        res1 = keep.tile([P, V], F32, name="res1")
-        nc.vector.tensor_tensor(rr23[:], rr23[:], cnt_t[:].unsqueeze(1).to_broadcast([P, 2, V]), ALU.mult)
-        nc.vector.tensor_tensor(rr1[:], rr1[:], cnt_t[:], ALU.mult)
-        nc.vector.tensor_scalar(res23[:], rr23[:], -1.0, one[:], ALU.mult, ALU.add)
-        nc.vector.tensor_scalar(res1[:], rr1[:], -1.0, one[:], ALU.mult, ALU.add)
-        nc.sync.dma_start(out[2 * P:4 * P, :].rearrange("(n p) v -> p n v", p=P), res23[:])
-        nc.sync.dma_start(out[P:2 * P, :], res1[:])
+        rr = {}
+        for n in (0, 2, 3):
+            rr[n] = keep.tile([P, V], F32, name="rr%d" % n)
+            largest(rr[n][:], tb[n])
+            decay(rr[n][:], rr[n][:], n)
+        rr[1] = keep.tile([P, V], F32, name="rr1", tag="best13", align_bytes=64)
+        largest(rr[1][:], wide)
+        res = {n: keep.tile([P, V], F32, name="res%d" % n) for n in rr}
+        nc.gpsimd.tensor_tensor(rr[0][:], rr[0][:], cnt_t[:], ALU.mult)
+        nc.gpsimd.tensor_scalar(res[0][:], rr[0][:], -1.0, 1.0, ALU.mult, ALU.add)
+        for n in (2, 3, 1):
+            nc.vector.tensor_tensor(rr[n][:], rr[n][:], cnt_t[:], ALU.mult)
+        for n in (2, 3, 1):
+            nc.vector.tensor_scalar(res[n][:], rr[n][:], -1.0, one[:], ALU.mult, ALU.add)
+        for n in rr:
+            nc.sync.dma_start(out[P * n:P * (n + 1), :], res[n][:])

@@ -26,12 +26,16 @@ SIDES = 2
 SIDE = 4
 
 XS_FROM = 4
-ES_FROM = 16
+ES_FROM = 48
+NB_AT = P - 1
 WARM_UPS = 2
 
-ES_C_AT = 2048
-EW_B_AT = ES_C_AT + 64 - 2048
-HS_AT = ES_C_AT + 64
+NB_TAB_AT = 0
+WS0_AT = 8192
+XS_TAB_AT = WS0_AT + 512 - 64
+ES_C_AT = XS_TAB_AT + 64
+HS_AT = ES_C_AT
+EW_B_AT = ES_C_AT + 1024 - 64
 
 
 def tile_picked_ycham_dens_p_kernel(
@@ -45,30 +49,23 @@ def tile_picked_ycham_dens_p_kernel(
 
         offs_t = keep.tile([P, S // 16], U16, name="offs_t")
         oth_t = keep.tile([P, U // 16], U16, name="oth_t")
-        xs_tab = keep.tile([P, T], U8, name="xs_tab", align_bytes=64)
+        xs_tab = reuse.tile([P, T], U8, name="xs_tab", offset=XS_TAB_AT, align_bytes=64)
         es_tab = keep.tile([P, W], U8, name="es_tab", align_bytes=64)
-        nb_tab = keep.tile([P, W], F32, name="nb_tab", align_bytes=64)
+        nb_tab = reuse.tile([P, W], F32, name="nb_tab", offset=NB_TAB_AT, align_bytes=64)
         xw_tab = [keep.tile([P, T], I32, name="xw_tab%d" % g, align_bytes=64) for g in range(PASSES)]
         ew_tab = keep.tile([P, W], I32, name="ew_tab", align_bytes=64)
-        w_raw = [
-            reuse.tile([P, PACK, H], F32, name="w_raw0", offset=0, align_bytes=64),
-            keep.tile([P, PACK, H], F32, name="w_raw1", align_bytes=64),
-        ]
+        w_raw = [keep.tile([P, PACK, H], F32, name="w_raw%d" % g, align_bytes=64) for g in range(PASSES)]
         own_t = keep.tile([P, S // P], F32, name="own_t")
         cnt_t = keep.tile([P, V], F32, name="cnt_t")
-        ident = keep.tile([P, P], F32, name="ident", align_bytes=64)
         zero = keep.tile([P, 1], F32, name="zero")
-        es_d = keep.tile([P, SIDES, SIDE * V], U8, name="es_d", align_bytes=64)
         one = keep.tile([P, 1], F32, name="one")
 
-        nc.vector.memset(es_tab[:].bitcast(I32), 0)
-        nc.vector.memset(nb_tab[:].bitcast(I32), 0)
-        nc.vector.memset(xs_tab[:].bitcast(I32), 0)
         nc.vector.memset(zero[:], 0.0)
-        nc.vector.memset(ident[:], 0.0)
-        nc.vector.memset(es_d[:].bitcast(I32), 0)
+        nc.vector.memset(nb_tab[0:NB_AT, :].bitcast(I32), 0)
+        nc.vector.memset(xs_tab[:].bitcast(I32), 0)
+        nc.vector.memset(es_tab[0:ES_FROM, :].bitcast(I32), 0)
+        nc.vector.memset(es_tab[ES_FROM + 16:P, :].bitcast(I32), 0)
         nc.scalar.activation(one[:], zero[:], ACT.Exp)
-        make_identity(nc, ident[:], nomemset=True)
 
         def load_w(g):
             nc.sync.dma_start(w_raw[g][:], w1[512 * g:512 * (g + 1), :].rearrange("(p j) c -> p j c", j=PACK))
@@ -77,10 +74,10 @@ def tile_picked_ycham_dens_p_kernel(
             nc.sync.dma_start(tab[:], words.rearrange("p n t -> p (n t)").bitcast(I32))
 
         nc.sync.dma_start(oth_t[:], oth)
-        nc.sync.dma_start(offs_t[:], offs)
+        nc.sync.dma_start(nb_tab[NB_AT:P, :], nb[0:1, :])
         nc.sync.dma_start(es_tab[ES_FROM:ES_FROM + 16, :].bitcast(I32), e_scales[0].bitcast(I32))
         load_w(0)
-        nc.scalar.dma_start(nb_tab[0:1, :], nb[0:1, :])
+        nc.sync.dma_start(offs_t[:], offs)
         for quad in range(4):
             rows = slice(32 * quad + XS_FROM, 32 * quad + XS_FROM + 4 * PASSES)
             nc.sync.dma_start(xs_tab[rows, :].bitcast(I32), x_scales[:, 4 * quad:4 * quad + 4, :].bitcast(I32))
@@ -95,7 +92,6 @@ def tile_picked_ycham_dens_p_kernel(
         nbg = keep.tile([P, U], F32, name="nbg", align_bytes=64)
         xw = [keep.tile([P, S], U32, name="xw%d" % g, align_bytes=64) for g in range(PASSES)]
         w_bf = [keep.tile([P, PACK, P, PACK], BF16, name="w_bf%d" % g, align_bytes=64) for g in range(PASSES)]
-        ws = [keep.tile([P, H], U8, name="ws%d" % g, align_bytes=64) for g in range(PASSES)]
         h_bf = [keep.tile([P, HALF, PACK], BF16, name="h_bf%d" % a, align_bytes=64) for a in range(2)]
         hc = [keep.tile([P, HALF], U32, name="hc%d" % a, align_bytes=64) for a in range(2)]
 
@@ -114,12 +110,21 @@ def tile_picked_ycham_dens_p_kernel(
                 wc[g][:, cols].bitcast(FP8X4), ws[g][:, cols], w_bf[g][:, first:last].rearrange("p r m j -> p (r m j)")
             )
 
-        nc.vector.tensor_copy(nbg[:], nb_tab[:].indirect(oth_t[:]))
+        nc.scalar.activation(nbg[:], nb_tab[:].indirect(oth_t[:]), ACT.Copy, scale=-1.0)
+        es_d = reuse.tile([P, SIDES, SIDE * V], U8, name="es_d", offset=NB_TAB_AT, align_bytes=64)
+        ident = reuse.tile([P, P], F32, name="ident", offset=NB_TAB_AT + U, align_bytes=64)
+        nc.gpsimd.memset(es_d[:].bitcast(I32), 0)
+        make_identity(nc, ident[:])
         cast_w(0)
         cast_w(1)
-        quant_w(0, 0, 4)
+        nc.vector.tensor_copy(xs[:], xs_tab[:].indirect(offs_t[:]))
         es_c = reuse.tile([P, SIDES, SIDE * V], U8, name="es_c", offset=ES_C_AT, align_bytes=64)
         nc.vector.tensor_copy(es_c[:].bitcast(I32), es_rows[:].bitcast(I32).rearrange("p (v c) -> p c v", c=SIDES))
+        ws = [
+            reuse.tile([P, H], U8, name="ws0", offset=WS0_AT, align_bytes=64),
+            keep.tile([P, H], U8, name="ws1", align_bytes=64),
+        ]
+        quant_w(0, 0, 4)
         for quad in range(4):
             nc.sync.dma_start(
                 es_d[32 * quad:32 * quad + 4].rearrange("p c v -> p (c v)").bitcast(I32),
@@ -136,7 +141,6 @@ def tile_picked_ycham_dens_p_kernel(
                 rhs=wc[0][:].bitcast(FP8X4), rhs_scale=ws[0][:],
                 start=True, stop=True,
             )
-        nc.vector.tensor_copy(xs[:], xs_tab[:].indirect(offs_t[:]))
         quant_w(1, 0, 2)
         nc.vector.tensor_copy(xw[0][:], xw_tab[0][:].bitcast(U32).indirect(offs_t[:]))
         quant_w(1, 2, 4)
@@ -145,15 +149,13 @@ def tile_picked_ycham_dens_p_kernel(
                 xw[1][:, P * first:P * last], xw_tab[1][:].bitcast(U32).indirect(offs_t[:, 8 * first:8 * last])
             )
 
-        nb_row = keep.tile([1, P, SIDES, QUARTERS], F32, name="nb_row", tag="w_raw1", align_bytes=64)
-        for c in range(SIDES):
-            nc.scalar.activation(
-                nb_row[:, :, c, :].rearrange("o (u e) q -> o u e q", e=SIDE),
-                nbg[0:1, :].rearrange("o (q u c e) -> o c u e q", q=QUARTERS, c=SIDES, e=SIDE)[:, c],
-                ACT.Copy, scale=-1.0,
-            )
+        nb_row = keep.tile([P, P, SIDES, QUARTERS], F32, name="nb_row", tag="w_raw1", align_bytes=64)
+        nc.scalar.copy(
+            nb_row[96:P].rearrange("p (u e) c q -> p u c q e", e=SIDE),
+            nbg[96:P, :].rearrange("p (q u c e) -> p u c q e", q=QUARTERS, c=SIDES, e=SIDE),
+        )
         neg_nb = keep.tile([P, SIDES, QUARTERS], F32, name="neg_nb", align_bytes=64)
-        nc.sync.dma_start(neg_nb[:].rearrange("p c q -> p (c q)"), nb_row[:].rearrange("o m c q -> o m (c q)"))
+        nc.sync.dma_start(neg_nb[:].rearrange("p c q -> p (c q)"), nb_row[NB_AT:P].rearrange("o m c q -> o m (c q)"))
 
         def first_product(hb, n, g, r, start, stop):
             cols = slice(P * n, P * (n + 1))

@@ -28,7 +28,7 @@ SIDE = 4
 XS_FROM = 4
 ES_FROM = 48
 NB_AT = P - 1
-WARM_UPS = 2
+WARM_UPS = 3
 
 NB_TAB_AT = 0
 WS0_AT = 8192
@@ -74,7 +74,7 @@ def tile_picked_ycham_dens_p_kernel(
             nc.sync.dma_start(tab[:], words.rearrange("p n t -> p (n t)").bitcast(I32))
 
         nc.sync.dma_start(oth_t[:], oth)
-        nc.sync.dma_start(nb_tab[NB_AT:P, :], nb[0:1, :])
+        nc.scalar.dma_start(nb_tab[NB_AT:P, :], nb[0:1, :])
         nc.sync.dma_start(es_tab[ES_FROM:ES_FROM + 16, :].bitcast(I32), e_scales[0].bitcast(I32))
         load_w(0)
         nc.sync.dma_start(offs_t[:], offs)
@@ -133,16 +133,19 @@ def tile_picked_ycham_dens_p_kernel(
         nc.sync.dma_start(cnt_t[:], cnt)
         with nc.allow_non_contiguous_dma(reason="one value a partition and token block"):
             nc.sync.dma_start(own_t[:], own.rearrange("(n p) o -> p (n o)", p=P))
-        warm = psum.tile([P, BANK], F32, name="warm", tag="bank4")
+        warm = psum.tile([P, HALF], F32, name="warm", tag="bank4")
         for r in range(WARM_UPS):
             nc.tensor.matmul_mx(
                 warm[:],
                 lhsT=wc[0][:, P * r:P * (r + 1)].bitcast(FP8X4), lhsT_scale=ws[0][:, P * r:P * (r + 1)],
-                rhs=wc[0][:].bitcast(FP8X4), rhs_scale=ws[0][:],
+                rhs=wc[0][:, 0:HALF].bitcast(FP8X4), rhs_scale=ws[0][:, 0:HALF],
                 start=True, stop=True,
             )
         quant_w(1, 0, 2)
-        nc.vector.tensor_copy(xw[0][:], xw_tab[0][:].bitcast(U32).indirect(offs_t[:]))
+        for a in range(2):
+            nc.vector.tensor_copy(
+                xw[0][:, HALF * a:HALF * (a + 1)], xw_tab[0][:].bitcast(U32).indirect(offs_t[:, 16 * a:16 * (a + 1)])
+            )
         quant_w(1, 2, 4)
         for first, last in ((0, 1), (1, 2), (2, 4)):
             nc.vector.tensor_copy(

@@ -28,6 +28,7 @@ SIDE = 4
 XS_FROM = 4
 ES_FROM = 48
 NB_AT = P - 1
+AHEAD = 3
 WARM_UPS = 3
 
 NB_TAB_AT = 0
@@ -104,6 +105,12 @@ def tile_picked_ycham_dens_p_kernel(
                     w_raw[g][:].rearrange("p j (m r) -> p m j r", r=PACK)[:, :, :, r:r + 2],
                 )
 
+        def gather_xw(g):
+            for first, last in ((0, 1), (1, 2), (2, 4)):
+                nc.vector.tensor_copy(
+                    xw[g][:, P * first:P * last], xw_tab[g][:].bitcast(U32).indirect(offs_t[:, 8 * first:8 * last])
+                )
+
         def quant_w(g, first, last):
             cols = slice(P * first, P * last)
             nc.vector.quantize_mx(
@@ -142,15 +149,9 @@ def tile_picked_ycham_dens_p_kernel(
                 start=True, stop=True,
             )
         quant_w(1, 0, 2)
-        for a in range(2):
-            nc.vector.tensor_copy(
-                xw[0][:, HALF * a:HALF * (a + 1)], xw_tab[0][:].bitcast(U32).indirect(offs_t[:, 16 * a:16 * (a + 1)])
-            )
+        gather_xw(0)
         quant_w(1, 2, 4)
-        for first, last in ((0, 1), (1, 2), (2, 4)):
-            nc.vector.tensor_copy(
-                xw[1][:, P * first:P * last], xw_tab[1][:].bitcast(U32).indirect(offs_t[:, 8 * first:8 * last])
-            )
+        gather_xw(1)
 
         nb_row = keep.tile([P, P, SIDES, QUARTERS], F32, name="nb_row", tag="w_raw1", align_bytes=64)
         nc.scalar.copy(
@@ -171,7 +172,7 @@ def tile_picked_ycham_dens_p_kernel(
 
         for n in range(S // P):
             hb = psum.tile([P, BANK], F32, name="hb", tag="bank%d" % n)
-            if n < HALF // P:
+            if n < AHEAD:
                 for g in range(PASSES):
                     for r in range(PACK):
                         first_product(hb, n, g, r, (g, r) == (0, 0), (g, r) == (PASSES - 1, PACK - 1))

@@ -98,12 +98,11 @@ def tile_picked_ycham_dens_p_kernel(
 
         wc = [keep.tile([P, H], U32, name="wc%d" % g, align_bytes=64) for g in range(PASSES)]
 
-        def cast_w(g):
-            for r in (0, 2):
-                nc.scalar.copy(
-                    w_bf[g][:, r:r + 2].rearrange("p r m j -> p m j r"),
-                    w_raw[g][:].rearrange("p j (m r) -> p m j r", r=PACK)[:, :, :, r:r + 2],
-                )
+        def cast_w(g, r, first, last):
+            nc.scalar.copy(
+                w_bf[g][:, r:r + 2, first:last].rearrange("p r m j -> p m j r"),
+                w_raw[g][:].rearrange("p j (m r) -> p m j r", r=PACK)[:, first:last, :, r:r + 2],
+            )
 
         def gather_xw(g):
             for first, last in ((0, 1), (1, 2), (2, 4)):
@@ -122,8 +121,11 @@ def tile_picked_ycham_dens_p_kernel(
         ident = reuse.tile([P, P], F32, name="ident", offset=NB_TAB_AT + U, align_bytes=64)
         nc.gpsimd.memset(es_d[:].bitcast(I32), 0)
         make_identity(nc, ident[:])
-        cast_w(0)
-        cast_w(1)
+        cast_w(0, 0, 0, P)
+        cast_w(0, 2, 0, P)
+        cast_w(1, 2, 0, P // 2)
+        cast_w(1, 0, 0, P)
+        cast_w(1, 2, P // 2, P)
         nc.vector.tensor_copy(xs[:], xs_tab[:].indirect(offs_t[:]))
         es_c = reuse.tile([P, SIDES, SIDE * V], U8, name="es_c", offset=ES_C_AT, align_bytes=64)
         nc.vector.tensor_copy(es_c[:].bitcast(I32), es_rows[:].bitcast(I32).rearrange("p (v c) -> p c v", c=SIDES))
@@ -148,9 +150,9 @@ def tile_picked_ycham_dens_p_kernel(
                 rhs=wc[0][:, 0:HALF].bitcast(FP8X4), rhs_scale=ws[0][:, 0:HALF],
                 start=True, stop=True,
             )
-        quant_w(1, 0, 2)
         gather_xw(0)
-        quant_w(1, 2, 4)
+        quant_w(1, 0, 2)
+        quant_w(1, 2, PACK)
         gather_xw(1)
 
         nb_row = keep.tile([P, P, SIDES, QUARTERS], F32, name="nb_row", tag="w_raw1", align_bytes=64)

@@ -50,7 +50,7 @@ def tile_picked_ycham_dens_p_kernel(
 
         offs_t = keep.tile([P, S // 16], U16, name="offs_t")
         oth_t = keep.tile([P, U // 16], U16, name="oth_t")
-        xs_tab = reuse.tile([P, T], U8, name="xs_tab", offset=XS_TAB_AT, align_bytes=64)
+        xs_tab = reuse.tile([P, 2, T], U8, name="xs_tab", offset=XS_TAB_AT, align_bytes=64)
         es_tab = keep.tile([P, W], U8, name="es_tab", align_bytes=64)
         nb_tab = reuse.tile([P, W], F32, name="nb_tab", offset=NB_TAB_AT, align_bytes=64)
         xw_tab = [keep.tile([P, T], I32, name="xw_tab%d" % g, align_bytes=64) for g in range(PASSES)]
@@ -63,7 +63,7 @@ def tile_picked_ycham_dens_p_kernel(
 
         nc.vector.memset(zero[:], 0.0)
         nc.vector.memset(nb_tab[0:NB_AT, :].bitcast(I32), 0)
-        nc.vector.memset(xs_tab[:].bitcast(I32), 0)
+        nc.vector.memset(xs_tab[:].rearrange("p s n -> p (s n)").bitcast(I32), 0)
         nc.vector.memset(es_tab[0:ES_FROM, :].bitcast(I32), 0)
         nc.vector.memset(es_tab[ES_FROM + 16:P, :].bitcast(I32), 0)
         nc.scalar.activation(one[:], zero[:], ACT.Exp)
@@ -79,9 +79,13 @@ def tile_picked_ycham_dens_p_kernel(
         nc.sync.dma_start(es_tab[ES_FROM:ES_FROM + 16, :].bitcast(I32), e_scales[0].bitcast(I32))
         load_w(0)
         nc.sync.dma_start(offs_t[:], offs)
-        for quad in range(4):
-            rows = slice(32 * quad + XS_FROM, 32 * quad + XS_FROM + 4 * PASSES)
-            nc.sync.dma_start(xs_tab[rows, :].bitcast(I32), x_scales[:, 4 * quad:4 * quad + 4, :].bitcast(I32))
+        for g in range(PASSES):
+            for low in (0, 64):
+                rows = slice(low + XS_FROM + 4 * g, low + XS_FROM + 4 * g + 4)
+                nc.sync.dma_start(
+                    xs_tab[rows].bitcast(I32),
+                    x_scales[g, low // 8:low // 8 + 8, :].rearrange("(s r) n -> r s n", s=2).bitcast(I32),
+                )
         load_w(1)
         load_words(xw_tab[0], x_words[0])
         load_words(xw_tab[1], x_words[1])
@@ -126,7 +130,11 @@ def tile_picked_ycham_dens_p_kernel(
         cast_w(1, 2, 0, P // 2)
         cast_w(1, 0, 0, P)
         cast_w(1, 2, P // 2, P)
-        nc.vector.tensor_copy(xs[:], xs_tab[:].indirect(offs_t[:]))
+        for low in (0, 64):
+            nc.vector.tensor_copy(
+                xs_tab[low + 32:low + 64, 0, :].bitcast(I32), xs_tab[low:low + 32, 1, :].bitcast(I32)
+            )
+        nc.vector.tensor_copy(xs[:], xs_tab[:, 0, :].indirect(offs_t[:]))
         es_c = reuse.tile([P, SIDES, SIDE * V], U8, name="es_c", offset=ES_C_AT, align_bytes=64)
         nc.vector.tensor_copy(es_c[:].bitcast(I32), es_rows[:].bitcast(I32).rearrange("p (v c) -> p c v", c=SIDES))
         ws = [

@@ -34,7 +34,7 @@ WARM_UPS = 3
 NB_TAB_AT = 0
 WS0_AT = 8192
 XS_TAB_AT = WS0_AT + 512 - 64
-ES_C_AT = XS_TAB_AT + 64
+ES_C_AT = XS_TAB_AT + 2048
 HS_AT = ES_C_AT
 EW_B_AT = ES_C_AT + 1024 - 64
 
@@ -74,9 +74,9 @@ def tile_picked_ycham_dens_p_kernel(
         def load_words(tab, words):
             nc.sync.dma_start(tab[:], words.rearrange("p n t -> p (n t)").bitcast(I32))
 
-        nc.sync.dma_start(oth_t[:], oth)
-        nc.scalar.dma_start(nb_tab[NB_AT:P, :], nb[0:1, :])
         nc.sync.dma_start(es_tab[ES_FROM:ES_FROM + 16, :].bitcast(I32), e_scales[0].bitcast(I32))
+        nc.sync.dma_start(oth_t[:], oth)
+        nc.sync.dma_start(nb_tab[NB_AT:P, :], nb[0:1, :])
         load_w(0)
         nc.sync.dma_start(offs_t[:], offs)
         for g in range(PASSES):
@@ -91,8 +91,8 @@ def tile_picked_ycham_dens_p_kernel(
         load_words(xw_tab[1], x_words[1])
         load_words(ew_tab, e_words[0])
 
-        es_rows = keep.tile([P, U], U8, name="es_rows", align_bytes=64)
-        nc.vector.tensor_copy(es_rows[:], es_tab[:].indirect(oth_t[:]))
+        es_c = reuse.tile([P, SIDES, SIDE * V], U8, name="es_c", offset=ES_C_AT, align_bytes=64)
+        nc.vector.tensor_copy(es_c[:].rearrange("p c (v e) -> p v c e", e=SIDE), es_tab[:].indirect(oth_t[:]))
         xs = keep.tile([P, S], U8, name="xs", align_bytes=64)
         nbg = keep.tile([P, U], F32, name="nbg", align_bytes=64)
         xw = [keep.tile([P, S], U32, name="xw%d" % g, align_bytes=64) for g in range(PASSES)]
@@ -135,8 +135,6 @@ def tile_picked_ycham_dens_p_kernel(
                 xs_tab[low + 32:low + 64, 0, :].bitcast(I32), xs_tab[low:low + 32, 1, :].bitcast(I32)
             )
         nc.vector.tensor_copy(xs[:], xs_tab[:, 0, :].indirect(offs_t[:]))
-        es_c = reuse.tile([P, SIDES, SIDE * V], U8, name="es_c", offset=ES_C_AT, align_bytes=64)
-        nc.vector.tensor_copy(es_c[:].bitcast(I32), es_rows[:].bitcast(I32).rearrange("p (v c) -> p c v", c=SIDES))
         ws = [
             reuse.tile([P, H], U8, name="ws0", offset=WS0_AT, align_bytes=64),
             keep.tile([P, H], U8, name="ws1", align_bytes=64),

@@ -74,9 +74,9 @@ def tile_picked_ycham_dens_p_kernel(
         def load_words(tab, words):
             nc.sync.dma_start(tab[:], words.rearrange("p n t -> p (n t)").bitcast(I32))
 
-        nc.sync.dma_start(es_tab[ES_FROM:ES_FROM + 16, :].bitcast(I32), e_scales[0].bitcast(I32))
         nc.sync.dma_start(oth_t[:], oth)
-        nc.sync.dma_start(nb_tab[NB_AT:P, :], nb[0:1, :])
+        nc.scalar.dma_start(nb_tab[NB_AT:P, :], nb[0:1, :])
+        nc.sync.dma_start(es_tab[ES_FROM:ES_FROM + 16, :].bitcast(I32), e_scales[0].bitcast(I32))
         load_w(0)
         nc.sync.dma_start(offs_t[:], offs)
         for g in range(PASSES):

from contextlib import ExitStack

import concourse.mybir as mybir
from concourse.masks import make_identity

K, T, S, H, V, W, U = 1024, 1024, 512, 512, 128, 2048, 1024
FLOPS = 2 * K * H * S + 2 * H * S * U

F32 = mybir.dt.float32
BF16 = mybir.dt.bfloat16
I32 = mybir.dt.int32
U32 = mybir.dt.uint32
U16 = mybir.dt.uint16
U8 = mybir.dt.uint8
FP8X4 = mybir.dt.float8_e4m3fn_x4
ALU = mybir.AluOpType
ACT = mybir.ActivationFunctionType

P = 128
PACK = 4
PASSES = K // (P * PACK)
BANK = 512
HALF = S // 2
QUARTERS = 4
SIDES = 2
SIDE = 4

XS_FROM = 4
ES_FROM = 48
NB_AT = P - 1
AHEAD = 3
WARM_UPS = 3

NB_TAB_AT = 0
WS0_AT = 8192
XS_TAB_AT = WS0_AT + 512 - 64
ES_C_AT = XS_TAB_AT + 2048
HS_AT = ES_C_AT
EW_B_AT = ES_C_AT + 1024 - 64


def tile_picked_ycham_dens_p_kernel(
    tc, x_words, x_scales, w1, e_words, e_scales, nb, own, cnt, offs, oth, out
):
    nc = tc.nc
    with ExitStack() as ctx:
        keep = ctx.enter_context(tc.tile_pool(name="keep", bufs=1))
        reuse = ctx.enter_context(tc.tile_pool(name="reuse", bufs=1))
        psum = ctx.enter_context(tc.psum_pool(name="psum", bufs=1))

        offs_t = keep.tile([P, S // 16], U16, name="offs_t")
        oth_t = keep.tile([P, U // 16], U16, name="oth_t")
        xs_tab = reuse.tile([P, 2, T], U8, name="xs_tab", offset=XS_TAB_AT, align_bytes=64)
        es_tab = keep.tile([P, W], U8, name="es_tab", align_bytes=64)
        nb_tab = reuse.tile([P, W], F32, name="nb_tab", offset=NB_TAB_AT, align_bytes=64)
        xw_tab = [keep.tile([P, T], I32, name="xw_tab%d" % g, align_bytes=64) for g in range(PASSES)]
        ew_tab = keep.tile([P, W], I32, name="ew_tab", align_bytes=64)
        w_raw = [keep.tile([P, PACK, H], F32, name="w_raw%d" % g, align_bytes=64) for g in range(PASSES)]
        own_t = keep.tile([P, S // P], F32, name="own_t")
        cnt_t = keep.tile([P, V], F32, name="cnt_t")
        zero = keep.tile([P, 1], F32, name="zero")
        one = keep.tile([P, 1], F32, name="one")

        nc.vector.memset(zero[:], 0.0)
        nc.vector.memset(nb_tab[0:NB_AT, :].bitcast(I32), 0)
        nc.vector.memset(xs_tab[:].rearrange("p s n -> p (s n)").bitcast(I32), 0)
        nc.vector.memset(es_tab[0:ES_FROM, :].bitcast(I32), 0)
        nc.vector.memset(es_tab[ES_FROM + 16:P, :].bitcast(I32), 0)
        nc.scalar.activation(one[:], zero[:], ACT.Exp)

        def load_w(g):
            nc.sync.dma_start(w_raw[g][:], w1[512 * g:512 * (g + 1), :].rearrange("(p j) c -> p j c", j=PACK))

        def load_words(tab, words):
            nc.sync.dma_start(tab[:], words.rearrange("p n t -> p (n t)").bitcast(I32))

        nc.sync.dma_start(oth_t[:], oth)
        nc.scalar.dma_start(nb_tab[NB_AT:P, :], nb[0:1, :])
        nc.sync.dma_start(es_tab[ES_FROM:ES_FROM + 16, :].bitcast(I32), e_scales[0].bitcast(I32))
        load_w(0)
        nc.sync.dma_start(offs_t[:], offs)
        for g in range(PASSES):
            for low in (0, 64):
                rows = slice(low + XS_FROM + 4 * g, low + XS_FROM + 4 * g + 4)
                nc.sync.dma_start(
                    xs_tab[rows].bitcast(I32),
                    x_scales[g, low // 8:low // 8 + 8, :].rearrange("(s r) n -> r s n", s=2).bitcast(I32),
                )
        load_w(1)
        load_words(xw_tab[0], x_words[0])
        load_words(xw_tab[1], x_words[1])
        load_words(ew_tab, e_words[0])

        es_c = reuse.tile([P, SIDES, SIDE * V], U8, name="es_c", offset=ES_C_AT, align_bytes=64)
        nc.vector.tensor_copy(es_c[:].rearrange("p c (v e) -> p v c e", e=SIDE), es_tab[:].indirect(oth_t[:]))
        xs = keep.tile([P, S], U8, name="xs", align_bytes=64)
        nbg = keep.tile([P, U], F32, name="nbg", align_bytes=64)
        xw = [keep.tile([P, S], U32, name="xw%d" % g, align_bytes=64) for g in range(PASSES)]
        w_bf = [keep.tile([P, PACK, P, PACK], BF16, name="w_bf%d" % g, align_bytes=64) for g in range(PASSES)]
        h_bf = [keep.tile([P, HALF, PACK], BF16, name="h_bf%d" % a, align_bytes=64) for a in range(2)]
        hc = [keep.tile([P, HALF], U32, name="hc%d" % a, align_bytes=64) for a in range(2)]

        wc = [keep.tile([P, H], U32, name="wc%d" % g, align_bytes=64) for g in range(PASSES)]

        def cast_w(g, r, first, last):
            nc.scalar.copy(
                w_bf[g][:, r:r + 2, first:last].rearrange("p r m j -> p m j r"),
                w_raw[g][:].rearrange("p j (m r) -> p m j r", r=PACK)[:, first:last, :, r:r + 2],
            )

        def gather_xw(g):
            for first, last in ((0, 1), (1, 2), (2, 4)):
                nc.vector.tensor_copy(
                    xw[g][:, P * first:P * last], xw_tab[g][:].bitcast(U32).indirect(offs_t[:, 8 * first:8 * last])
                )

        def quant_w(g, first, last):
            cols = slice(P * first, P * last)
            nc.vector.quantize_mx(
                wc[g][:, cols].bitcast(FP8X4), ws[g][:, cols], w_bf[g][:, first:last].rearrange("p r m j -> p (r m j)")
            )

        nc.scalar.activation(nbg[:], nb_tab[:].indirect(oth_t[:]), ACT.Copy, scale=-1.0)
        es_d = reuse.tile([P, SIDES, SIDE * V], U8, name="es_d", offset=NB_TAB_AT, align_bytes=64)
        ident = reuse.tile([P, P], F32, name="ident", offset=NB_TAB_AT + U, align_bytes=64)
        nc.gpsimd.memset(es_d[:].bitcast(I32), 0)
        make_identity(nc, ident[:])
        cast_w(0, 0, 0, P)
        cast_w(0, 2, 0, P)
        cast_w(1, 2, 0, P // 2)
        cast_w(1, 0, 0, P)
        cast_w(1, 2, P // 2, P)
        for low in (0, 64):
            nc.vector.tensor_copy(
                xs_tab[low + 32:low + 64, 0, :].bitcast(I32), xs_tab[low:low + 32, 1, :].bitcast(I32)
            )
        nc.vector.tensor_copy(xs[:], xs_tab[:, 0, :].indirect(offs_t[:]))
        ws = [
            reuse.tile([P, H], U8, name="ws0", offset=WS0_AT, align_bytes=64),
            keep.tile([P, H], U8, name="ws1", align_bytes=64),
        ]
        quant_w(0, 0, 4)
        for quad in range(4):
            nc.sync.dma_start(
                es_d[32 * quad:32 * quad + 4].rearrange("p c v -> p (c v)").bitcast(I32),
                es_c[ES_FROM + 4 * quad:ES_FROM + 4 * quad + 4].rearrange("p c v -> p (c v)").bitcast(I32),
            )
        nc.sync.dma_start(cnt_t[:], cnt)
        with nc.allow_non_contiguous_dma(reason="one value a partition and token block"):
            nc.sync.dma_start(own_t[:], own.rearrange("(n p) o -> p (n o)", p=P))
        warm = psum.tile([P, HALF], F32, name="warm", tag="bank4")
        for r in range(WARM_UPS):
            nc.tensor.matmul_mx(
                warm[:],
                lhsT=wc[0][:, P * r:P * (r + 1)].bitcast(FP8X4), lhsT_scale=ws[0][:, P * r:P * (r + 1)],
                rhs=wc[0][:, 0:HALF].bitcast(FP8X4), rhs_scale=ws[0][:, 0:HALF],
                start=True, stop=True,
            )
        gather_xw(0)
        quant_w(1, 0, 2)
        quant_w(1, 2, PACK)
        gather_xw(1)

        nb_row = keep.tile([P, P, SIDES, QUARTERS], F32, name="nb_row", tag="w_raw1", align_bytes=64)
        nc.scalar.copy(
            nb_row[96:P].rearrange("p (u e) c q -> p u c q e", e=SIDE),
            nbg[96:P, :].rearrange("p (q u c e) -> p u c q e", q=QUARTERS, c=SIDES, e=SIDE),
        )
        neg_nb = keep.tile([P, SIDES, QUARTERS], F32, name="neg_nb", align_bytes=64)
        nc.sync.dma_start(neg_nb[:].rearrange("p c q -> p (c q)"), nb_row[NB_AT:P].rearrange("o m c q -> o m (c q)"))

        def first_product(hb, n, g, r, start, stop):
            cols = slice(P * n, P * (n + 1))
            nc.tensor.matmul_mx(
                hb[:, P * r:P * (r + 1)],
                lhsT=wc[g][:, P * r:P * (r + 1)].bitcast(FP8X4), lhsT_scale=ws[g][:, P * r:P * (r + 1)],
                rhs=xw[g][:, cols].bitcast(FP8X4), rhs_scale=xs[XS_FROM + 4 * g:P, cols],
                start=start, stop=stop,
            )

        for n in range(S // P):
            hb = psum.tile([P, BANK], F32, name="hb", tag="bank%d" % n)
            if n < AHEAD:
                for g in range(PASSES):
                    for r in range(PACK):
                        first_product(hb, n, g, r, (g, r) == (0, 0), (g, r) == (PASSES - 1, PACK - 1))
            else:
                for r in range(PACK):
                    for g in range(PASSES):
                        first_product(hb, n, g, r, g == 0, g == PASSES - 1)
            nc.scalar.copy(
                h_bf[n // 2][:, P * (n % 2):P * (n % 2 + 1), :],
                hb[:].rearrange("p (r t) -> p t r", r=PACK),
            )

        def quant_h(a):
            scales = reuse.tile([P, HALF], U8, name="hs%d" % a, offset=HS_AT + HALF * a, align_bytes=64)
            nc.vector.quantize_mx(hc[a][:].bitcast(FP8X4), scales[:], h_bf[a][:].rearrange("p t r -> p (t r)"))
            return scales

        def gather_ew(words, first, last):
            nc.vector.tensor_copy(
                words.rearrange("p c (v e) -> p v c e", e=SIDE),
                ew_tab[:].bitcast(U32).indirect(oth_t[:, 16 * first:16 * last]),
            )

        ew_a = keep.tile([P, SIDES, 2 * P], U32, name="ew_a", align_bytes=64)
        gather_ew(ew_a[:], 0, 2)
        hs0 = quant_h(0)
        ew_b = reuse.tile([P, 2, SIDES, P], U32, name="ew_b", offset=EW_B_AT, align_bytes=64)
        for q in (2, 3):
            gather_ew(ew_b[:, q - 2], q, q + 1)
        hs = [hs0, quant_h(1)]
        ew_d = [ew_a[:, :, 0:P], ew_a[:, :, P:2 * P], ew_b[:, 0], ew_b[:, 1]]

        best = {}
        for a in range(2):
            for q in range(QUARTERS):
                yb = psum.tile([P, SIDES, HALF], F32, name="yb", tag="bank%d" % (q + QUARTERS * (1 - a)))
                for c in range(SIDES):
                    nc.tensor.matmul_mx(
                        yb[:, c, :],
                        lhsT=ew_d[q][:, c, :].bitcast(FP8X4), lhsT_scale=es_d[:, c, P * q:P * (q + 1)],
                        rhs=hc[a][:].bitcast(FP8X4), rhs_scale=hs[a][:],
                        start=True, stop=True,
                    )
                best[a, q] = keep.tile([P, HALF], F32, name="best%d%d" % (a, q), align_bytes=64)
                nc.scalar.activation(best[a, q][:], yb[:, 0, :], ACT.Identity, bias=neg_nb[:, 0, q:q + 1])
                nc.vector.scalar_tensor_tensor(
                    best[a, q][:], yb[:, 1, :], neg_nb[:, 1, q:q + 1], best[a, q][:], ALU.add, ALU.max
                )

        def turn(n):
            tb = psum.tile([P, BANK], F32, name="tb", tag="bank%d" % (QUARTERS + n if n else 0))
            for q in range(QUARTERS):
                nc.tensor.transpose(tb[:, P * q:P * (q + 1)], best[n // 2, q][:, P * (n % 2):P * (n % 2 + 1)], ident[:])
            return tb

        def largest(dst, src):
            nc.vector.tensor_reduce(dst, src[:].rearrange("p (v e) -> p v e", e=SIDE), mybir.AxisListType.X, ALU.max)

        def decay(dst, src, n):
            nc.scalar.activation(dst, src, ACT.Relu, scale=-1.0, bias=own_t[:, n:n + 1])
            nc.scalar.activation(dst, dst, ACT.Exp, scale=-1.0)

        tb = [turn(n) for n in range(S // P)]
        wide = reuse.tile([P, BANK], F32, name="wide", offset=EW_B_AT, align_bytes=64)
        decay(wide[:], tb[1][:], 1)
        rr = {}
        for n in (0, 2, 3):
            rr[n] = keep.tile([P, V], F32, name="rr%d" % n)
            largest(rr[n][:], tb[n])
            decay(rr[n][:], rr[n][:], n)
        rr[1] = keep.tile([P, V], F32, name="rr1", tag="best13", align_bytes=64)
        largest(rr[1][:], wide)
        res = {n: keep.tile([P, V], F32, name="res%d" % n) for n in rr}
        nc.gpsimd.tensor_tensor(rr[0][:], rr[0][:], cnt_t[:], ALU.mult)
        nc.gpsimd.tensor_scalar(res[0][:], rr[0][:], -1.0, 1.0, ALU.mult, ALU.add)
        for n in (2, 3, 1):
            nc.vector.tensor_tensor(rr[n][:], rr[n][:], cnt_t[:], ALU.mult)
        for n in (2, 3, 1):
            nc.vector.tensor_scalar(res[n][:], rr[n][:], -1.0, one[:], ALU.mult, ALU.add)
        for n in rr:
            nc.sync.dma_start(out[P * n:P * (n + 1), :], res[n][:])
